import numpy as np, ml_dtypes
CORES = [23,119,17,113]
N = 4
import mx_ref
BF = ml_dtypes.bfloat16
def pick(q, e):
    c = np.concatenate([q[0].reshape(128, -1, 4), np.zeros((128, 1, 4), np.uint8)], axis=1); s = np.concatenate([q[1], np.ones((16, 1), np.uint8)], axis=1)
    return (np.ascontiguousarray(c[:, e].reshape(128, -1)), np.ascontiguousarray(s[:, e]))
def join(*qs):
    return (np.concatenate([q[0] for q in qs], axis=1), np.concatenate([q[1] for q in qs], axis=1))
def put(q, e, v):
    c, s = q[0].reshape(128, -1, 4).copy(), q[1].copy(); c[:, e] = v[0].reshape(128, -1, 4); s[:, e] = v[1]
    return (c.reshape(128, -1), s)
def pk(c, s):
    return (np.ascontiguousarray(c), mx_ref.live(s))
def emit(q):
    return q[0], q[1]
def tile(rs):
    return np.stack(rs, axis=2).reshape(128, -1).astype(BF)
def cut(t, i, w=512):
    return t[:, w * i:w * i + w]
def f(rng, *shape):
    return mx_ref.flush((rng.standard_normal(shape, dtype=np.float32) * np.exp2(rng.integers(-2, 3, shape[:-1] + (1,)))).astype(BF))
def wide(rng, *shape, cols=0):
    v = rng.standard_normal(shape, dtype=np.float32) * np.exp2(rng.integers(-12, 13, shape)).astype(np.float32)
    if cols: v *= np.repeat(np.exp2(rng.integers(-cols, cols + 1, shape[:-2] + (1, shape[-1] // 4))) * (rng.random(shape[:-2] + (1, shape[-1] // 4)) > 0.0625), 4, axis=-1).astype(np.float32)
    return mx_ref.flush(v.astype(BF))
P, CAPP, L, CB = 256, 128, 2, 128
def big(v, k):
    v = v.astype(np.float32) * np.float32(k)
    v[np.abs(v) < np.float32(2.0 ** -10)] = 0
    return v.astype(BF)
def number(z):
    n = np.zeros(z.shape[1], np.int64)
    for b in range(L): n += (z[b] < 0) * (1 << b)
    return n
def buckets(x, pl):
    X = [mx_ref.quantize(np.ascontiguousarray(x[s])) for s in range(N)]
    return X, np.stack([number(mx_ref.matmul(mx_ref.quantize(np.ascontiguousarray(pl[s])), X[s])) for s in range(N)])
def taken(bk):
    at = np.full((N, N, CAPP), -1)
    for d in range(N):
        for s in range(N):
            e = np.flatnonzero(bk[s] == d)[:CAPP]
            at[d, s, :e.size] = e
    return at
def attend(c, wv, e):
    e = np.concatenate([e, np.setdiff1d(np.arange(512), e)[:max(4 - len(e), len(e) % 2)]])
    m = pick(c, e)
    ct = [pick(c, np.arange(t, 512, 4)) for t in range(4)]
    A = tile([np.float32(0.0625) * np.maximum(mx_ref.matmul(k, m) + np.float32(0), np.float32(0)) for k in ct])
    qw = mx_ref.quantize(np.ascontiguousarray(wv))
    V = tile([mx_ref.matmul(k, qw) for k in ct])
    qa = mx_ref.quantize(A)
    O = [mx_ref.matmul(mx_ref.quantize(np.ascontiguousarray(cut(V, i))), qa) for i in range(4)]
    h = np.zeros((128, 512, 4), BF)
    h[:, e] = tile([np.float32(0.0625) * o for o in O]).reshape(128, -1, 4)
    return A, V, h.reshape(128, 2048)
def planes(rng):
    p = np.array(f(rng, 128, 512))
    p[:, 4 * L:] = 0
    return np.stack([p] * N)
def plain(rng):
    return {"x": big(f(rng, N, 128, 4 * P), 0.25), "pl": planes(rng), "p2": planes(rng), "wv": big(f(rng, N, 128, 2048), 0.25), "w": f(rng, N, 128, 512)}
def aimed(rng, d, want, gone=0, then=None, two=None):
    x, p = d["x"].astype(np.float32).reshape(N, 128, P, 4), np.zeros((128, 128, 4), np.float32)
    gone = np.zeros((N, P), np.int64) + gone
    at = rng.permutation(128)[:16 * L + 16].reshape(L + 1, 16)
    side = np.zeros((N, 128, 4), np.float32)
    for b in range(L):
        v = (1 + rng.random((16, 4))) * rng.choice([-1.0, 1.0], (16, 4))
        p[at[b], b] = v
        turn = (1 - 2 * (want >> b & 1)) * (1 - (gone >> b & 1))
        x[:, at[b]] = np.abs(x[:, at[b]]) * (np.sign(v)[None, :, None, :] * turn[:, None, :, None]) * (0.0625 if then is None else 1.0)
        side[:, at[b]] = np.sign(v)[None] * (1 - 2 * (np.arange(N) >> b & 1))[:, None, None]
    parted = np.zeros((128, 4), np.float32)
    if two is not None:
        k = two[2][:, None, :, None]
        u = rng.choice([-1.0, 1.0], (16, 4))
        parted[at[L]] = u
        x = np.where(k != 0, np.float32(0.125) * x, x)
        x[:, at[L]] = np.where(k != 0, 0.5 * (1 + rng.random((N, 16, P, 4))) * u[None, :, None, :] * k, x[:, at[L]])
    x = x * (gone != N - 1)[:, None, :, None]
    d = {**d, "x": big(x.reshape(N, 128, 4 * P), 1), "pl": np.stack([p.reshape(128, 512).astype(BF)] * N)}
    if then is None: return d
    p2, wv = np.zeros((128, 128, 4), np.float32), d["wv"].astype(np.float32).reshape(N, 128, 4, 128, 4)
    on = rng.permutation(128)[:16 * L].reshape(L, 16)
    for b in range(L):
        p2[on[b], b] = 1 + rng.random((16, 4))
        for q in range(N):
            sign = parted if two is not None and q == two[0] and b == two[1] else side[q]
            wv[q][:, :, on[b]] = np.abs(wv[q][:, :, on[b]]) * sign[:, None, None, :] * (1 - 2 * (int(then[q]) >> b & 1))
    return {**d, "wv": big(wv.reshape(N, 128, 2048), 1), "p2": np.stack([p2.reshape(128, 512).astype(BF)] * N)}
def setup_inputs(rng):
    return plain(rng)
def setup_inputs_crowd(rng):
    h, g = (int(v) for v in rng.permutation(N)[:2])
    c, then = rng.permutation(N), np.zeros(N, np.int64)
    then[c] = np.roll(c, 1)
    bit = int(rng.choice([b for b in range(L) if int(then[h]) ^ (1 << b) != h]))
    one = int(rng.choice([q for q in range(N) if q not in (h, g) and int(then[q]) != int(then[h]) ^ (1 << bit)]))
    others = np.delete(np.arange(N), [h, g, one])
    o, n = rng.permutation(N), np.full(N, CAPP)
    n[o[N // 2:]] += rng.integers(1, P - CAPP + 1, N - N // 2)
    n[o[-1]] = P
    r, more = int(o[N // 2]), P // (CAPP + 1) - 1
    if more: n[r] = rng.integers(CAPP + 1, P - more * (CAPP + 1) + 1)
    want = rng.choice(others, (N, P))
    for s in range(N): want[s, rng.permutation(P)[:n[s]]] = h
    e = rng.permutation(np.flatnonzero((want != h) & (np.arange(N) != r)[:, None]))
    want.flat[e[:CB]] = g
    want.flat[e[CB]] = one
    if more:
        e = rng.permutation(np.flatnonzero(want[r] != h))
        want[r, e[:more * (CAPP + 1)]] = np.repeat(rng.choice(others, more, replace=False), CAPP + 1)
    kind = np.zeros((N, P), np.int64)
    for s in range(N):
        e = np.flatnonzero(want[s] == h)
        kind[s, e] = 1 - 2 * ((np.arange(e.size) + int(rng.integers(0, 2))) % 2)
    return aimed(rng, plain(rng), want, then=then, two=(h, bit, kind))
def setup_inputs_few(rng):
    o = rng.permutation(N)
    want = rng.choice(o[2:], (N, P))
    want[int(rng.integers(0, N)), int(rng.integers(0, P))] = o[0]
    return aimed(rng, plain(rng), want)
def setup_inputs_neg(rng):
    d, g = plain(rng), rng.permutation(16)
    want = np.stack([rng.permutation(P) % N for s in range(N)])
    part = 8 * g[:, None] + np.arange(8)
    rows = (4 * part[L:].reshape(-1)[:, None] + np.arange(4)).reshape(-1)
    x, p = np.zeros((N, P, 512)), np.zeros((128, 128, 4))
    for b in range(L):
        v = rng.choice([-1.0, 1.0], (8, 4))
        p[part[b], b] = v * (1 + rng.random((8, 4)))
        e = (4 * part[b][:, None] + np.arange(4)).reshape(-1)
        x[:, :, e] = 2.0 ** -8 * v.reshape(-1) * (1 - 2 * (want >> b & 1))[:, :, None]
    for q in range(N):
        s, i = np.nonzero(want == q)
        v = np.full((P, P), -2.0 ** -7)
        v[np.arange(P), np.arange(P)] = P * 2.0 ** -7
        x[s[:, None], i[:, None], rng.permutation(rows)[:P][None, :]] = v * rng.choice([-1.0, 1.0], P)
    x *= np.exp2(rng.integers(-1, 2, (N, P, 1)))
    x = np.ascontiguousarray(x.reshape(N, P, 128, 4).transpose(0, 2, 1, 3)).reshape(N, 128, 4 * P)
    return {**d, "x": x.astype(np.float32).astype(BF), "pl": np.stack([p.reshape(128, 512).astype(np.float32).astype(BF)] * N)}
def setup_inputs_zero(rng):
    gone = np.zeros((N, P), np.int64)
    for s in range(N):
        e = rng.permutation(P)
        gone[s, e[:P // 4]] = N - 1
        gone[s, e[P // 4:P // 2]] = 1 << rng.integers(0, L, P // 2 - P // 4)
    d = aimed(rng, plain(rng), rng.integers(0, N, (N, P)), gone)
    b, q, on = int(rng.integers(0, L)), int(rng.integers(0, N)), rng.permutation(128)[:16]
    p2, wv = np.array(d["p2"]).reshape(N, 128, 128, 4), np.array(d["wv"]).reshape(N, 128, 4, 128, 4)
    p2[:, np.setdiff1d(np.arange(128), on), b] = 0
    wv[q][:, :, on] = 0
    return {**d, "p2": p2.reshape(N, 128, 512), "wv": wv.reshape(N, 128, 2048)}
def setup_inputs_spread(rng):
    return {**plain(rng), "x": big(wide(rng, N, 128, 4 * P, cols=2), 2.0 ** -10)}
def check_inputs(d):
    b = []
    for k in ("x", "pl", "p2", "wv", "w"):
        v = np.abs(d[k].astype(np.float32))
        if not (np.isfinite(v).all() and ((v == 0) | (v >= 2.0 ** -30) & (v <= 2.0 ** 30)).all()): b.append("a value of " + k)
    for k in ("pl", "p2"):
        p = d[k].astype(np.float32)
        if (p[:, :, 4 * L:] != 0).any(): b.append(k + " has numbers behind its first L columns")
        if (p != p[:1]).any(): b.append(k + " isn't the same on all ranks")
    return b
def reference(x, pl, p2, wv, w):
    X, bk = buckets(x, pl)
    at = taken(bk)
    H, num, to = [], [], []
    for d in range(N):
        c = join(*[pick(X[s], at[d, s]) for s in range(N)])
        A, V, h = attend(c, wv[d], np.flatnonzero(at[d].reshape(-1) >= 0))
        h = mx_ref.quantize(h)
        n = np.concatenate([np.where(at[d, s] >= 0, P * s + at[d, s], -1) for s in range(N)])
        H.append(h)
        num.append(n)
        to.append(np.where(n >= 0, number(mx_ref.matmul(mx_ref.quantize(np.ascontiguousarray(p2[d])), h)), -1))
    H = join(*H)
    num = np.concatenate(num + [np.full(1, -1)])
    oc, osc = np.zeros((N, 128, 4 * N * CB), np.uint8), np.zeros((N, 16, N * CB), np.uint8)
    nb, y = np.zeros((N, 1, N * CB), np.float32), np.zeros((N, 128, N * CB), np.float32)
    for e in range(N):
        k = np.full(N * CB, -1)
        for d in range(N):
            i = np.flatnonzero(to[d] == e)[:CB]
            k[d * CB + np.arange(i.size)] = 512 * d + i
        h = pick(H, k)
        oc[e], osc[e] = emit(h)
        nb[e, 0] = num[k]
        y[e] = mx_ref.matmul(mx_ref.quantize(np.ascontiguousarray(w[e])), h)
    return {"oc": oc, "osc": osc, "id": nb, "y": y}

@@ -1,0 +1,523 @@
+from concourse.bass import DstId, RemoteDMATransfer
+from concourse.mybir import dt, AluOpType, AxisListType, ActivationFunctionType
+
+F, B, I, U = "float32", "bfloat16", "int32", "uint16"
+Q, S8 = "float8_e4m3fn_x4", "uint8"
+COL = {n: ("ki", k) for k, n in enumerate(("pc", "b2", "b3", "b4", "qi", "gi"))}
+COL.update({n: ("kf", k) for k, n in enumerate(("t0a", "t1a", "t0b", "h16", "q4", "gf", "cnt0", "cnt1"))})
+SCRATCH = {}
+for _n, _w, _t in (
+        ("plb", 8, B), ("p2b", 8, B), ("p1f", 8, F), ("p2f", 8, F), ("xb", 1024, B), ("wvb", 2048, B), ("wb", 512, B),
+        ("w1t", 1024, B), ("zt", 576, B), ("w2t", 1152, B), ("at", 2048, B), ("vt", 2048, B), ("ht", 2048, B),
+        ("sa0", 16, B), ("sa1", 16, B), ("sb0", 32, B), ("sb1", 32, B), ("hm", 32, B),
+        ("val1", 128, B), ("val2", 256, B), ("win1", 1040, B), ("win2", 2320, B), ("ki", 16, I), ("kf", 24, F),
+        ("vb1", 128, F), ("ctb", 32, F), ("plc", 256, F), ("c8", 32, F), ("dm1", 32, F), ("f8", 32, F), ("q16", 64, F),
+        ("dm2", 64, F), ("f16", 64, F), ("io2", 128, B), ("nadd", 32, F), ("X", 64, F), ("xt", 64, F), ("fF", 32, F),
+        ("nf", 32, F), ("nt", 32, F), ("ntt", 32, F), ("tb2", 256, B), ("am", 288, B), ("a1", 32, F), ("a2", 64, F),
+        ("c64", 16, F), ("dmp", 16, F), ("tabrow", 520, F), ("tab", 520, F),
+        ("g1", 256, B), ("ind1", 256, B), ("C1", 256, B), ("tI1", 256, B), ("tC1", 256, B), ("M1", 32, F), ("R1", 32, F),
+        ("l1", 32, F), ("l2", 32, F),
+        ("g2", 256, B), ("ind2", 416, B), ("C2", 416, B), ("J2", 256, B), ("tJ2", 256, B), ("tC2", 416, B), ("D2", 64, F),
+        ("M2", 64, F), ("R2", 64, F), ("dst2", 16, F),
+        ("pd", 32, F), ("pds", 32, F), ("gm", 64, F), ("gms", 64, F), ("idp", 32, F),
+        ("idt", 32, F), ("yb", 512, F),
+        ("do1", 8, U), ("do2", 16, U), ("off1", 32, U), ("off2", 32, U), ("offct", 32, U), ("offD", 4, U), ("nl", 32, U),
+        ("idu", 4, U), ("idl", 32, U)):
+    SCRATCH[_n] = ("sbuf", [128, _w], _t)
+for _n in ("wd1", "t21", "wd2", "t22"):
+    SCRATCH[_n] = ("sbuf", [128, 32, 32], B)
+for _n, _w in (("w1", 256), ("xq", 384), ("slota", 384), ("landa", 512), ("ct", 512), ("wvq", 512), ("aq", 512), ("vq", 512),
+               ("w2", 288), ("hq", 640), ("slotb", 384), ("landb", 512), ("wq", 128)):
+    SCRATCH[_n + "c"] = ("sbuf", [128, _w], Q)
+    SCRATCH[_n + "s"] = ("sbuf", [128, _w], S8)
+for _k in range(8):
+    SCRATCH["ps%d" % _k] = ("psum", [128, 512], F)
+
+SEMAPHORES = (["sv", "sa", "sp", "sg", "sent", "c1", "n1", "n2", "lpl", "lx0", "lx1", "lp2", "lwv", "lw", "ltb"]
+              + ["%s_%d" % (n, k) for n in ("c2", "s2") for k in range(4)]
+              + ["%s%d" % (n, k) for n in ("oc", "os", "yy", "ii") for k in range(4)])
+
+TINY = 2.0 ** -120
+LOW, FAR = -2.0 ** 99, 2.0 ** 20
+LIST1, LIST2 = 4, 260
+
+
+def rank_program(g, core, T, topo):
+    rank = T.rank_of(core)
+    if rank is None:
+        return
+    N = len(T.cores)
+    A, ACT = AluOpType, ActivationFunctionType
+    eng = {"v": g.vector, "a": g.scalar, "p": g.tensor, "g": g, "s": g.sync}
+    csem = {"v": "sv", "a": "sa", "p": "sp", "g": "sg"}
+    total, waited, know, acc = {}, {}, {q: {} for q in eng}, {}
+
+    def clash(x, y):
+        if x[1] >= y[2] or y[1] >= x[2]:
+            return False
+        if x[3] == y[3] and x[3] > 1:
+            a, b = x[1] % x[3], y[1] % y[3]
+            return a < b + y[4] and b < a + x[4]
+        return True
+
+    def order(q, tok):
+        sem, n, clock = tok
+        k = know[q]
+        if k.get(sem, 0) < n:
+            eng[q].wait_ge(T.sem[sem], n)
+            waited[sem] = max(waited.get(sem, 0), n)
+            k[sem] = n
+        for s, m in clock.items():
+            if k.get(s, 0) < m:
+                k[s] = m
+
+    def touch(q, reads, writes):
+        todo = []
+        for kind, specs in ((0, reads), (1, writes)):
+            for sp in specs:
+                for old, okind, tok, oq in acc.get(sp[0], ()):
+                    if sp[0][:2] == "ps":
+                        if oq != q:
+                            todo.append(tok)
+                    elif (kind or okind) and clash(sp, old):
+                        todo.append(tok)
+        todo.sort(key=lambda t: (t[0], -t[1]))
+        for t in todo:
+            order(q, t)
+
+    def note(q, tok, reads, writes):
+        for kind, specs in ((0, reads), (1, writes)):
+            for sp in specs:
+                acc.setdefault(sp[0], []).append((sp, kind, tok, q))
+
+    def v2(name, a, b, step=1):
+        return (T[name][:, a:b:step] if step > 1 else T[name][:, a:b], [(name, a, b, step, 1)], [])
+
+    def half(name, h):
+        return v2(name, 128 * h, 128 * h + 128)
+
+    def one(n):
+        return v2(COL[n][0], COL[n][1], COL[n][1] + 1)
+
+    def v3(name, a, b, c, d):
+        w = SCRATCH[name][1][2]
+        return (T[name][:, a:b, c:d], [(name, a * w + c, (b - 1) * w + d, w, d - c)], [])
+
+    def v3i(name, a, b, c):
+        w = SCRATCH[name][1][2]
+        return (T[name][:, a:b, c], [(name, a * w + c, (b - 1) * w + c + 1, w, 1)], [])
+
+    def codes(name, a, b, bits=None):
+        ap = T[name + "c"][:, a:b]
+        return (ap.bitcast(bits) if bits else ap, [(name + "c", a, b, 1, 1)], [])
+
+    def plane(name, a, b):
+        return v2(name + "s", a, b)
+
+    def by(win, off):
+        return (win[0].indirect(off[0]), win[1], off[1])
+
+    calls = {"tensor_copy": g.vector.tensor_copy, "tensor_tensor": g.vector.tensor_tensor, "memset": g.vector.memset,
+             "tensor_reduce": g.vector.tensor_reduce, "tensor_scalar": g.vector.tensor_scalar,
+             "tensor_tensor_scan": g.vector.tensor_tensor_scan, "transpose": g.vector.transpose,
+             "quantize_mx": g.vector.quantize_mx, "activation": g.scalar.activation, "matmul_mx": g.tensor.matmul_mx,
+             "iota": g.iota, "partition_broadcast": g.partition_broadcast}
+
+    def do(q, call, *args, outs=1, **kw):
+        reads, writes, plain = [], [], []
+        for i, x in enumerate(args):
+            if isinstance(x, tuple):
+                (writes if i < outs else reads).extend(x[1])
+                reads.extend(x[2])
+                plain.append(x[0])
+            else:
+                plain.append(x)
+        for k in kw:
+            if isinstance(kw[k], tuple):
+                reads.extend(kw[k][1])
+                kw[k] = kw[k][0]
+        touch(q, reads, writes)
+        s = csem[q]
+        calls[call](*plain, **kw).then_inc(T.sem[s], 1)
+        total[s] = total.get(s, 0) + 1
+        note(q, (s, total[s], dict(know[q])), reads, writes)
+
+    def dma(q, sem, out, in_):
+        touch(q, in_[1], out[1])
+        eng[q].dma_start(out[0], in_[0]).then_inc(T.sem[sem], 16)
+        total[sem] = 16
+        note(q, (sem, 16, dict(know[q])), in_[1], out[1])
+
+    def ext(ap):
+        return (ap, [], [])
+
+    def arrive(sem, n, *specs):
+        total[sem] = n
+        for sp in specs:
+            note("far", (sem, n, {}), [], sp[1])
+
+    def tt(out, a, b, op):
+        do("v", "tensor_tensor", out, a, b, op)
+
+    def ts(out, a, s1, op0, s2=None, op1=None):
+        if op1 is None:
+            do("v", "tensor_scalar", out, a, s1, None, op0)
+        else:
+            do("v", "tensor_scalar", out, a, s1, s2, op0, op1)
+
+    def cp(out, a):
+        do("v", "tensor_copy", out, a)
+
+    def act(out, a, f, **kw):
+        do("a", "activation", out, a, f, **kw)
+
+    def fill(out, c):
+        do("v", "memset", out, c)
+
+    def scan(out, a, b, init, op0, op1):
+        do("v", "tensor_tensor_scan", out, a, b, init, op0, op1)
+
+    def turn32(out, a):
+        do("v", "transpose", out, a)
+
+    def total_of(out, a):
+        do("v", "tensor_reduce", out, a, AxisListType.X, A.add)
+
+    def quant(name, a, b, tile, lo):
+        do("v", "quantize_mx", codes(name, a, b), plane(name, a, b), v2(tile, lo, lo + 4 * (b - a)), outs=2)
+
+    def mm(bank, n, l, la, r, ra, start=True, stop=True):
+        do("p", "matmul_mx", v2("ps%d" % bank, 0, n), codes(l, la, la + 128), plane(l, la, la + 128),
+           codes(r, ra, ra + n), plane(r, ra, ra + n), start, stop)
+
+    def iota(out, pattern, base, cm, flag=True):
+        if flag:
+            do("g", "iota", out, pattern, base, cm, allow_small_or_imprecise_dtypes=True)
+        else:
+            do("g", "iota", out, pattern, base, cm)
+
+    off = [r for r in range(N) if r != rank and topo.chip(T.cores[r]) != topo.chip(core)]
+    near = [r for r in range(N) if r != rank and topo.chip(T.cores[r]) == topo.chip(core)]
+    perm = off + near + [rank]
+    share = {r: 8 if r in near else 4 for r in off + near}
+    every = sum(share.values())
+    used, mask = [], {}
+    for r in off + near:
+        es = [e for e in topo.engines(core, T.cores[r]) if e not in used][:share[r]]
+        used += es
+        mask[r] = sum(1 << e for e in es)
+    sent = [0]
+
+    def send(ks, sem, pairs):
+        trs = []
+        for k, (src, dst) in zip(ks, pairs):
+            touch("g", src[1], [])
+            rid, pid = topo.addr(T.cores[perm[k]])[:2]
+            trs.append(RemoteDMATransfer(dst_ids=[DstId(rid=rid, pnc=pid)], dma_engine_mask=mask[perm[k]],
+                                         remote_sem=T.sem[sem], src=src[0], dst=dst[0]))
+            sent[0] += share[perm[k]]
+        g.remote_dma_fused(trs, local_sem=T.sem.sent)
+
+    def send_cols(ks, sem, sem2, slot, land):
+        u8 = dt.uint8
+        send(ks, sem, [(codes(slot, 128 * k, 128 * k + 128, u8), codes(land, 128 * rank, 128 * rank + 128, u8)) for k in ks])
+        send(ks, sem2, [(plane(slot, 128 * k, 128 * k + 128), plane(land, 128 * rank, 128 * rank + 128)) for k in ks])
+
+    far_ks, near_ks = list(range(len(off))), list(range(len(off), N - 1))
+    all_ks = far_ks + near_ks
+
+    dma("s", "lpl", v2("plb", 0, 8), ext(T.pl[:, 0:8]))
+    dma("a", "lx0", v2("xb", 0, 512), ext(T.x[:, 0:512]))
+    dma("s", "lx1", v2("xb", 512, 1024), ext(T.x[:, 512:1024]))
+    touch("s", v2("xb", 0, 1024)[1], [])
+    dma("s", "lp2", v2("p2b", 0, 8), ext(T.p2[:, 0:8]))
+    dma("s", "lwv", v2("wvb", 0, 2048), ext(T.wv[:]))
+    dma("s", "lw", v2("wb", 0, 512), ext(T.w[:]))
+
+    iota(one("pc"), [[0, 1]], 0, 1, False)
+    iota(v2("sa1", 0, 16), [[0, 4], [-2, 2], [0, 2]], 1, 0)
+    iota(v2("sa0", 0, 16), [[0, 8], [-2, 2]], 1, 0)
+    iota(v2("vb1", 0, 128), [[32, 8], [1, 16]], -128, 0)
+    iota(v2("ctb", 0, 32), [[1, 4], [64, 8]], 0, 0)
+    iota(v2("c8", 0, 32), [[0, 4], [1, 8]], 0, 0)
+    iota(v2("q16", 0, 64), [[0, 4], [4, 16]], 0, 0)
+    iota(v2("nadd", 0, 32), [[256, 4], [0, 8]], 1, 0)
+    iota(v2("sb0", 0, 32), [[0, 16], [-2, 2]], 1, 0)
+    iota(v2("sb1", 0, 32), [[0, 8], [-2, 2], [0, 2]], 1, 0)
+    iota(v2("hm", 0, 32), [[0, 4], [-1, 2], [0, 4]], 1, 0)
+    iota(v2("c64", 0, 16), [[64, 16]], -1024, 0)
+
+    fill(v2("zt", 0, 576), 0.0)
+    fill(v2("w1t", 512, 1024), 0.0)
+    for n, sh in (("b4", 4), ("b3", 3)):
+        ts(one(n), one("pc"), sh, A.arith_shift_right, 1, A.bitwise_and)
+    ts(one("t1a"), one("b4"), TINY, A.mult)
+    ts(one("t0a"), one("b3"), TINY, A.mult)
+    ts(one("h16"), one("b4"), 16.0, A.mult)
+    quant("xq", 256, 384, "zt", 0)
+    fill(v2("a1", 0, 32), 0.25)
+    fill(v2("a1", 0, 32, 4), LOW)
+
+    def plane_cols(k, b, t):
+        return v2("w1t", 512 * b + t, 512 * b + 512, 32) if k == 1 else v2("w2t", 576 * b + 64 + t, 576 * b + 564, 16)
+
+    act(v2("w1t", 0, 512), v2("zt", 0, 512), ACT.Copy)
+    act(v2("p1f", 0, 8), v2("plb", 0, 8), ACT.Copy)
+    for t in range(4):
+        act(plane_cols(1, 0, t), v2("sa0", 0, 16), ACT.Copy, scale=v2("p1f", t, t + 1))
+    act(v2("val1", 0, 128), v2("vb1", 0, 128), ACT.Identity, bias=one("h16"))
+    act(v2("win1", LIST1, LIST1 + 516), v2("zt", 0, 516), ACT.Identity, bias=128.0)
+    for b in range(2):
+        act(v2("w2t", 576 * b, 576 * b + 576), v2("zt", 0, 576), ACT.Copy)
+    act(v2("ind2", 256, 416), v2("zt", 0, 160), ACT.Copy)
+    act(v2("am", 0, 288), v2("zt", 0, 288), ACT.Identity, bias=1.0)
+    act(v2("a2", 0, 64), v2("zt", 0, 64), ACT.Identity, bias=0.25)
+    for t in range(4):
+        ts(plane_cols(1, 1, t), v2("sa1", 0, 16), v2("plb", 4 + t, 5 + t), A.mult)
+
+    quant("w1", 128, 256, "w1t", 512)
+    quant("xq", 0, 128, "xb", 0)
+    quant("w1", 0, 128, "w1t", 0)
+    quant("xq", 128, 256, "xb", 512)
+    for h in range(2):
+        for b in (1, 0):
+            mm(2 * h + b, 128, "w1", 128 * b, "xq", 128 * h)
+    prod = lambda h, b: v2("ps%d" % (2 * h + b), 0, 128)
+
+    def gate(k, h):
+        o = half("g%d" % k, h)
+        if k == 1:
+            ts(o, prod(h, 1), one("t1a"), A.is_ge, LOW, A.mult)
+        else:
+            tt(o, prod(h, 1), half("tb2", h), A.is_ge)
+
+    def bound(k, h):
+        o = half("g%d" % k, h)
+        if k == 1:
+            ts(o, o, one("t0a"), A.add)
+        else:
+            ts(o, o, LOW, A.mult, one("t0b"), A.add)
+
+    def member(k, h):
+        tt(half("ind%d" % k, h), prod(h, 0), half("g%d" % k, h), A.is_lt)
+
+    def count1(h):
+        scan(half("C1", h), half("ind1", h), v2("zt", 0, 128), v2("C1", 127, 128) if h else 0.0, A.add, A.add)
+
+    gate(1, 0)
+    bound(1, 0)
+    gate(1, 1)
+    member(1, 0)
+    bound(1, 1)
+    count1(0)
+    member(1, 1)
+    turn32(half("tI1", 0), half("ind1", 0))
+    count1(1)
+    turn32(half("tC1", 0), half("C1", 0))
+    turn32(half("tI1", 1), half("ind1", 1))
+    turn32(half("tC1", 1), half("C1", 1))
+    tt(v2("M1", 0, 32), v2("tI1", 0, 256, 8), v2("tC1", 0, 256, 8), A.mult)
+    scan(v2("R1", 0, 32), v2("a1", 0, 32), v2("M1", 0, 32), 0.0, A.add, A.max)
+    ts(v2("do1", 0, 8), v2("R1", 3, 32, 4), 4.0, A.mult)
+    cp(by(v2("win1", 0, 1040), v2("do1", 0, 8)), v2("val1", 0, 128))
+
+    def spread(win, lo, wd):
+        for k in range(4):
+            for h in range(2):
+                o, z = v3(wd, 8 * k, 8 * k + 8, 16 * h, 16 * h + 16), v2(win, lo + perm[k], lo + perm[k] + 509, 4)
+                if k > 1 or k + h == 0:
+                    act(o, z, ACT.Copy)
+                else:
+                    cp(o, z)
+
+    def pick(dst, a, b, src, w, offs, k):
+        o = v2(offs, 8 * k, 8 * k + (b - a) // 16)
+        cp(codes(dst, a, b, dt.uint32), by(codes(src, 0, w, dt.uint32), o))
+        act(plane(dst, a, b), by(plane(src, 0, w), o), ACT.Copy)
+
+    spread("win1", LIST1, "wd1")
+    for hf in range(2):
+        a, b = 16 * hf, 16 * hf + 16
+        turn32(v3("t21", a, b, 0, 32), v3("wd1", a, b, 0, 32))
+        tt(v2("l1", a, b), v3i("t21", a, b, 0), v3i("t21", a, b, 16), A.add)
+        cp(v2("off1", a, b), v2("l1", a, b))
+        if hf == 0:
+            pick("slota", 0, 256, "xq", 384, "off1", 0)
+        else:
+            pick("slota", 256, 384, "xq", 384, "off1", 2)
+        send_cols(far_ks if hf == 0 else near_ks, "c1", "c1", "slota", "landa")
+    send(all_ks, "n1", [(v2("off1", 8 * k, 8 * k + 8), v2("nl", 8 * rank, 8 * rank + 8)) for k in all_ks])
+    pick("landa", 128 * rank, 128 * rank + 128, "xq", 384, "off1", 3)
+    cp(v2("nl", 8 * rank, 8 * rank + 8), v2("off1", 24, 32))
+
+    for h in range(2):
+        iota(half("plc", h), [[32, 4], [256, 2], [1, 16]], 128 * h - 256, 0)
+    iota(v2("io2", 0, 128), [[2, 128]], 0, 0)
+    iota(v2("win2", LIST2, LIST2 + 512), [[0, 512]], 256, 0)
+    for n, sh, m in (("b2", 2, 1), ("qi", 0, 15), ("gi", 4, 7)):
+        ts(one(n), one("pc"), sh, A.arith_shift_right, m, A.bitwise_and)
+    for b in range(2):
+        tt(v2("sb%d" % b, 0, 32), v2("sb%d" % b, 0, 32), v2("hm", 0, 32), A.mult)
+    ts(one("q4"), one("qi"), 4.0, A.mult)
+    ts(one("t0b"), one("b2"), TINY, A.mult)
+    cp(one("gf"), one("gi"))
+    ts(v2("am", 128, 129), one("b4"), -1.0, A.mult, 1.0, A.add)
+    fill(v2("a2", 0, 64, 4), LOW)
+    ts(v2("offct", 0, 32), v2("ctb", 0, 32), one("q4"), A.add)
+    act(v2("p2f", 0, 8), v2("p2b", 0, 8), ACT.Copy)
+    for b in range(2):
+        for t in range(4):
+            act(plane_cols(2, b, t), v2("sb%d" % b, 0, 32), ACT.Copy, scale=v2("p2f", 4 * b + t, 4 * b + t + 1))
+    act(v2("X", 0, 64), v2("zt", 0, 64), ACT.Identity, bias=8.0)
+    act(v2("f8", 0, 32), v2("c8", 0, 32), ACT.Sign)
+    act(v2("f16", 0, 64), v2("q16", 0, 64), ACT.Sign)
+    act(v2("tabrow", 512, 520), v2("zt", 0, 8), ACT.Copy)
+    act(v2("idp", 0, 32), v2("zt", 0, 32), ACT.Copy)
+    act(v2("val2", 0, 256), v2("plc", 0, 256), ACT.Identity, bias=one("h16"))
+    quant("wvq", 0, 512, "wvb", 0)
+    quant("w2", 0, 144, "w2t", 0)
+    quant("w2", 144, 288, "w2t", 576)
+    quant("hq", 512, 640, "zt", 0)
+    ts(v2("dmp", 0, 16), v2("c64", 0, 16), one("q4"), A.add, 0.0625, A.mult)
+    ts(v2("dm1", 0, 32), v2("c8", 0, 32), one("gf"), A.is_equal)
+    ts(v2("dm2", 0, 64), v2("q16", 0, 64), one("q4"), A.is_equal)
+
+    for s in range(N):
+        if s != rank:
+            arrive("c1", 2 * every, codes("landa", 128 * s, 128 * s + 128), plane("landa", 128 * s, 128 * s + 128))
+            arrive("n1", every, v2("nl", 8 * s, 8 * s + 8))
+    for t in range(4):
+        pick("ct", 128 * t, 128 * t + 128, "landa", 512, "offct", t)
+
+    def empty(q, tile, lo, t, bank, n, f):
+        o, z = v2(tile, lo + t, lo + 4 * n, 4), v2("ps%d" % bank, 0, n)
+        if f == "copy":
+            act(o, z, ACT.Copy) if q == "a" else cp(o, z)
+        elif f == "relu":
+            act(o, z, ACT.Relu, scale=0.0625) if q == "a" else ts(o, z, 0.0, A.max, 0.0625, A.mult)
+        else:
+            act(o, z, ACT.Copy, scale=0.0625) if q == "a" else ts(o, z, 0.0625, A.mult)
+
+    for t in range(4):
+        mm(t, 512, "ct", 128 * t, "wvq", 0)
+        empty("avav"[t], "vt", 0, t, t, 512, "copy")
+        if t == 1:
+            ts(v2("fF", 0, 32), v2("nl", 0, 32), 255.5, A.is_lt)
+            cp(v2("nf", 0, 32), v2("nl", 0, 32))
+            for m in range(4):
+                x = 32 * (m % 2) + 12 + 16 * (m // 2)
+                total_of(v2("X", x, x + 1), v2("fF", 8 * m, 8 * m + 8))
+            tt(v2("nt", 0, 32), v2("nf", 0, 32), v2("nadd", 0, 32), A.add)
+            turn32(v2("ntt", 0, 32), v2("nt", 0, 32))
+    dma("s", "ltb", (T.tabrow[0:1, 0:512], v2("tabrow", 0, 512)[1], []), (T.ntt[0:32, 0:16], v2("ntt", 0, 32)[1], []))
+    do("g", "partition_broadcast", v2("tab", 0, 520), (T.tabrow[0:1, 0:520], v2("tabrow", 0, 520)[1], []), 128)
+    quant("vq", 0, 512, "vt", 0)
+    for h, who in enumerate(("aaaa", "aaav")):
+        for t in range(4):
+            bank = 4 * (1 - h) + t
+            mm(bank, 256, "ct", 128 * t, "landa", 256 * h)
+            empty(who[t], "at", 1024 * h, t, bank, 256, "relu")
+        quant("aq", 256 * h, 256 * h + 256, "at", 1024 * h)
+    for lo, n, b0, who in ((0, 256, 4, "aava"), (256, 128, 0, "aaaa"), (384, 128, 4, "avav")):
+        for i in range(4):
+            mm(b0 + i, n, "vq", 128 * i, "aq", lo)
+        if lo == 384:
+            for b in (1, 0):
+                mm(b, 128, "w2", 144 * b + 16, "hq", 0, True, False)
+                mm(b, 128, "w2", 144 * b, "hq", 256, False, True)
+            for b in (1, 0):
+                mm(2 + b, 128, "w2", 144 * b + 16, "hq", 128, True, False)
+        for i in range(4):
+            empty(who[i], "ht", 4 * lo, i, b0 + i, n, "scale")
+        if lo == 0:
+            turn32(v2("xt", 0, 64), v2("X", 0, 64))
+            for h in range(2):
+                total_of(one("cnt%d" % h), v2("xt", 32 * h, 32 * h + 32))
+        quant("hq", lo, lo + n, "ht", 4 * lo)
+        if lo == 0:
+            for h in range(2):
+                ts(half("tb2", h), v2("io2", 0, 128), one("cnt%d" % h), A.is_lt, one("t0a"), A.mult)
+    for b in (1, 0):
+        mm(2 + b, 128, "w2", 144 * b, "hq", 384, False, True)
+
+    def sign(h):
+        act(half("J2", h), half("ind2", h), ACT.Identity, scale=2 * FAR, bias=-FAR)
+
+    gate(2, 0)
+    bound(2, 0)
+    gate(2, 1)
+    member(2, 0)
+    sign(0)
+    bound(2, 1)
+    scan(v2("C2", 0, 128), v2("am", 0, 128), v2("ind2", 0, 128), 0.0, A.mult, A.add)
+    member(2, 1)
+    sign(1)
+    turn32(v2("tC2", 0, 128), v2("C2", 0, 128))
+    scan(v2("C2", 128, 416), v2("am", 0, 288), v2("ind2", 128, 416), v2("C2", 127, 128), A.mult, A.add)
+    turn32(half("tJ2", 0), half("J2", 0))
+    turn32(half("tJ2", 1), half("J2", 1))
+    turn32(v2("tC2", 128, 416), v2("C2", 128, 416))
+    for h in range(2):
+        tt(v2("D2", 32 * h, 32 * h + 32), v2("tC2", 128 * h, 128 * h + 128, 4), v2("tC2", 272, 400, 4), A.add)
+    tt(v2("M2", 0, 64), v2("D2", 0, 64), v2("tJ2", 0, 256, 4), A.min)
+    scan(v2("R2", 0, 64), v2("a2", 0, 64), v2("M2", 0, 64), 0.0, A.add, A.max)
+    tt(v2("dst2", 0, 16), v2("R2", 3, 64, 4), v2("dmp", 0, 16), A.max)
+    ts(v2("do2", 0, 16), v2("dst2", 0, 16), 4.0, A.mult, 256.0, A.add)
+    cp(by(v2("win2", 0, 2320), v2("do2", 0, 16)), v2("val2", 0, 256))
+    spread("win2", LIST2, "wd2")
+    for hf in range(2):
+        a, b = 16 * hf, 16 * hf + 16
+        turn32(v3("t22", a, b, 0, 32), v3("wd2", a, b, 0, 32))
+        tt(v2("l2", a, b), v3i("t22", a, b, 0), v3i("t22", a, b, 16), A.add)
+        cp(v2("off2", a, b), v2("l2", a, b))
+        if hf == 0:
+            pick("slotb", 0, 256, "hq", 640, "off2", 0)
+        else:
+            tt(v2("pd", 0, 32), v2("l2", 0, 32), v2("dm1", 0, 32), A.mult)
+            pick("slotb", 256, 384, "hq", 640, "off2", 2)
+        send_cols(far_ks if hf == 0 else near_ks, "c2_%d" % rank, "s2_%d" % rank, "slotb", "landb")
+    scan(v2("pds", 0, 32), v2("f8", 0, 32), v2("pd", 0, 32), 0.0, A.mult, A.add)
+    cp(v2("offD", 0, 4), v2("pds", 7, 32, 8))
+    tt(v2("gm", 0, 64), by(v2("tab", 0, 520), v2("offD", 0, 4)), v2("dm2", 0, 64), A.mult)
+    scan(v2("gms", 0, 64), v2("f16", 0, 64), v2("gm", 0, 64), 0.0, A.mult, A.add)
+    cp(v2("idu", 0, 4), v2("gms", 15, 64, 16))
+    send(all_ks, "n2", [(v2("idu", k, k + 1), v2("idl", 8 * rank, 8 * rank + 1)) for k in all_ks])
+    pick("landb", 128 * rank, 128 * rank + 128, "hq", 640, "off2", 3)
+    cp(v2("idl", 8 * rank, 8 * rank + 1), v2("idu", 3, 4))
+    quant("wq", 0, 128, "wb", 0)
+
+    for s in range(N):
+        if s != rank:
+            arrive("c2_%d" % s, share[s], codes("landb", 128 * s, 128 * s + 128))
+            arrive("s2_%d" % s, share[s], plane("landb", 128 * s, 128 * s + 128))
+            arrive("n2", every, v2("idl", 8 * s, 8 * s + 1))
+    turn = [rank] + near + off
+
+    def store_codes(q, s):
+        dma(q, "oc%d" % s, ext(T.oc[:, 512 * s:512 * s + 512]), codes("landb", 128 * s, 128 * s + 128, dt.uint8))
+
+    for s in [rank] + off:
+        store_codes("s", s)
+    for i, s in enumerate(turn):
+        if s in near:
+            store_codes("a", s)
+        bank = (6, 7, 2, 3)[i]
+        mm(bank, 128, "wq", 0, "landb", 128 * s)
+        o, z = v2("yb", 128 * s, 128 * s + 128), v2("ps%d" % bank, 0, 128)
+        if i < 3:
+            act(o, z, ACT.Copy)
+        else:
+            cp(o, z)
+        dma("a" if i < 3 else "s", "yy%d" % s, ext(T.y[:, 128 * s:128 * s + 128]), o)
+    for k in range(4):
+        dma("a" if k % 2 else "s", "os%d" % k, ext(T.osc[4 * k:4 * k + 4, :]),
+            (T.landbs[32 * k:32 * k + 4, 0:512], plane("landb", 0, 512)[1], []))
+    ts(v2("idp", 0, 4), v2("idl", 0, 32, 8), -1.0, A.add)
+    turn32(v2("idt", 0, 32), v2("idp", 0, 32))
+    for s in range(N):
+        dma("a" if s % 2 else "s", "ii%d" % s, ext(T["id"][0:1, 128 * s:128 * s + 128]),
+            (T.idt[s:128:32, 0:32], v2("idt", 0, 32)[1], []))
+    total["sent"] = sent[0]
+    for sem in SEMAPHORES:
+        if total.get(sem, 0) > waited.get(sem, 0):
+            g.wait_ge(T.sem[sem], total[sem])

@@ -1,45 +1,49 @@
 from concourse.bass import DstId, RemoteDMATransfer
 from concourse.mybir import dt, AluOpType, AxisListType, ActivationFunctionType
 
-F, B, I, U = "float32", "bfloat16", "int32", "uint16"
+F, B, I, U, H = "float32", "bfloat16", "int32", "uint16", "float16"
 Q, S8 = "float8_e4m3fn_x4", "uint8"
-COL = {n: ("ki", k) for k, n in enumerate(("pc", "b2", "b3", "b4", "qi", "gi"))}
-COL.update({n: ("kf", k) for k, n in enumerate(("t0a", "t1a", "t0b", "h16", "q4", "gf", "cnt0", "cnt1"))})
-SCRATCH = {}
+COL = {n: ("ki", k) for k, n in enumerate(("pc", "pos", "b4", "m4", "qi", "gi", "p8", "r2", "r8", "b2"))}
+COL.update({n: ("kf", k) for k, n in enumerate(("tp", "nz", "kg", "k0", "kk", "lo", "h16", "c0", "c1", "q4", "gf", "mf",
+                                                "bf", "k2", "j0", "j1", "in1", "in2", "in3"))})
+SCRATCH = {"idd": ("dram", [4, 128, 1], F)}
 for _n, _w, _t in (
-        ("plb", 8, B), ("p2b", 8, B), ("p1f", 8, F), ("p2f", 8, F), ("xb", 1024, B), ("wvb", 2048, B), ("wb", 512, B),
-        ("w1t", 1024, B), ("zt", 576, B), ("w2t", 1152, B), ("at", 2048, B), ("vt", 2048, B), ("ht", 2048, B),
-        ("sa0", 16, B), ("sa1", 16, B), ("sb0", 32, B), ("sb1", 32, B), ("hm", 32, B),
-        ("val1", 128, B), ("val2", 256, B), ("win1", 1040, B), ("win2", 2320, B), ("ki", 16, I), ("kf", 24, F),
-        ("vb1", 128, F), ("ctb", 32, F), ("plc", 256, F), ("c8", 32, F), ("dm1", 32, F), ("f8", 32, F), ("q16", 64, F),
-        ("dm2", 64, F), ("f16", 64, F), ("io2", 128, B), ("nadd", 32, F), ("X", 64, F), ("xt", 64, F), ("fF", 32, F),
-        ("nf", 32, F), ("nt", 32, F), ("ntt", 32, F), ("tb2", 256, B), ("am", 288, B), ("a1", 32, F), ("a2", 64, F),
-        ("c64", 16, F), ("dmp", 16, F), ("tabrow", 520, F), ("tab", 520, F),
-        ("g1", 256, B), ("ind1", 256, B), ("C1", 256, B), ("tI1", 256, B), ("tC1", 256, B), ("M1", 32, F), ("R1", 32, F),
-        ("l1", 32, F), ("l2", 32, F),
-        ("g2", 256, B), ("ind2", 416, B), ("C2", 416, B), ("J2", 256, B), ("tJ2", 256, B), ("tC2", 416, B), ("D2", 64, F),
-        ("M2", 64, F), ("R2", 64, F), ("dst2", 16, F),
-        ("pd", 32, F), ("pds", 32, F), ("gm", 64, F), ("gms", 64, F), ("idp", 32, F),
-        ("idt", 32, F), ("yb", 512, F),
-        ("do1", 8, U), ("do2", 16, U), ("off1", 32, U), ("off2", 32, U), ("offct", 32, U), ("offD", 4, U), ("nl", 32, U),
-        ("idu", 4, U), ("idl", 32, U)):
+        ("plb", 8, B), ("p2b", 8, B), ("xb", 1024, B), ("wvb", 2048, B), ("wb", 512, B),
+        ("w1t", 1024, B), ("zt", 512, B), ("w2t", 1024, B), ("at", 2048, B), ("vt", 2048, B), ("ht", 2048, B),
+        ("sgn", 32, B), ("val1", 128, B), ("val2", 256, B), ("win1", 1808, B), ("win2", 1808, B), ("ki", 16, I),
+        ("kf", 24, F), ("io4", 4, F), ("vb1", 128, F), ("ctb", 32, F), ("plc", 256, F), ("c8", 32, F), ("dm1", 32, F),
+        ("f8", 32, F), ("q16", 64, F), ("dm2", 64, F), ("f16", 64, F), ("iof", 128, F), ("io2", 128, H),
+        ("ea", 4, F), ("eb", 4, F), ("ec", 4, F), ("tabrow", 520, F), ("tab", 520, F), ("msg", 16, F), ("nl", 16, F),
+        ("g1", 256, B), ("n1", 288, B), ("d1", 288, B), ("v1", 288, H), ("tn1", 256, B), ("tv1", 288, H), ("r1", 32, F),
+        ("l1", 32, F), ("l2", 32, F), ("pd1", 32, F), ("pe1", 32, F),
+        ("g2", 512, B), ("n2", 512, B), ("d2", 512, B), ("v2", 512, H), ("tn2", 512, B), ("tv2", 512, H), ("r2", 128, F),
+        ("pd", 32, F), ("pds", 32, F), ("gm", 64, F), ("gms", 64, F), ("yb", 512, F),
+        ("offg", 8, U), ("do1", 8, U), ("do2", 16, U), ("off1", 32, U), ("off2", 32, U), ("offct", 32, U), ("offD", 4, U)):
     SCRATCH[_n] = ("sbuf", [128, _w], _t)
 for _n in ("wd1", "t21", "wd2", "t22"):
     SCRATCH[_n] = ("sbuf", [128, 32, 32], B)
 for _n, _w in (("w1", 256), ("xq", 384), ("slota", 384), ("landa", 512), ("ct", 512), ("wvq", 512), ("aq", 512), ("vq", 512),
-               ("w2", 288), ("hq", 640), ("slotb", 384), ("landb", 512), ("wq", 128)):
+               ("w2", 256), ("hq", 640), ("slotb", 384), ("landb", 512), ("wq", 128)):
     SCRATCH[_n + "c"] = ("sbuf", [128, _w], Q)
     SCRATCH[_n + "s"] = ("sbuf", [128, _w], S8)
 for _k in range(8):
     SCRATCH["ps%d" % _k] = ("psum", [128, 512], F)
 
-SEMAPHORES = (["sv", "sa", "sp", "sg", "sent", "c1", "n1", "n2", "lpl", "lx0", "lx1", "lp2", "lwv", "lw", "ltb"]
+SEMAPHORES = (["sv", "sa", "sp", "sg", "sent", "c1", "m1", "m2", "lpl", "lx0", "lx1", "lp2", "lwv", "lw"]
               + ["%s_%d" % (n, k) for n in ("c2", "s2") for k in range(4)]
-              + ["%s%d" % (n, k) for n in ("oc", "os", "yy", "ii") for k in range(4)])
+              + ["%s%d" % (n, k) for n in ("oc", "os", "yy", "ii", "tb") for k in range(4)])
 
 TINY = 2.0 ** -120
-LOW, FAR = -2.0 ** 99, 2.0 ** 20
-LIST1, LIST2 = 4, 260
+HIGH = 2.0 ** 99
+TOP = 1792
+START = (768, 768, 512, 256)
+JUMP = (512.0, 640.0, 512.0, 512.0)
+
+PLAN = ("pc00 ps00 pc33 mV0 pc22 ps33 mV3 ps22 pc11 ps11 mV2 mV1 eV00v eV30a mA00 eV20v mA01 mA03 mA02 eA00a eV10v mA10 "
+        "eA03a mA13 tab eA01v mA12 qv0 mA11 eA02a qa0 mH01 eA10a eA13a mH02 mH00 eA12v fa2 eA11a qa1 eH02v mH03 mH11 mH13 "
+        "eH01a mH12 eH00a eH03v eH13v eH11a qh0 mH10 mH21 eH12a fa0 eH10a mH23 mH22 fa1 eH21a mH20 qh1 fa3 eH23a eH20a "
+        "mRa0 eH22a mRa1 gR0 mRb0 mRb1 gR1 nR0 qh2 mRb2 sR0 mRa2 tn0 cR1 nR1 sR1 gR2 cR2 tv0 nR2 sR2 tn1 uR0 tn2 cR3 tv1 "
+        "dR0 sR3 uR1 xR0 tv2 dR1 uR2 xR1 dR2 xR2").split()
 
 
 def rank_program(g, core, T, topo):
@@ -76,7 +80,7 @@ def rank_program(g, core, T, topo):
         for kind, specs in ((0, reads), (1, writes)):
             for sp in specs:
                 for old, okind, tok, oq in acc.get(sp[0], ()):
-                    if sp[0][:2] == "ps":
+                    if SCRATCH[sp[0]][0] == "psum":
                         if oq != q:
                             todo.append(tok)
                     elif (kind or okind) and clash(sp, old):
@@ -118,7 +122,7 @@ def rank_program(g, core, T, topo):
         return (win[0].indirect(off[0]), win[1], off[1])
 
     calls = {"tensor_copy": g.vector.tensor_copy, "tensor_tensor": g.vector.tensor_tensor, "memset": g.vector.memset,
-             "tensor_reduce": g.vector.tensor_reduce, "tensor_scalar": g.vector.tensor_scalar,
+             "tensor_scalar": g.vector.tensor_scalar,
              "tensor_tensor_scan": g.vector.tensor_tensor_scan, "transpose": g.vector.transpose,
              "quantize_mx": g.vector.quantize_mx, "activation": g.scalar.activation, "matmul_mx": g.tensor.matmul_mx,
              "iota": g.iota, "partition_broadcast": g.partition_broadcast}
@@ -180,15 +184,12 @@ def rank_program(g, core, T, topo):
     def turn32(out, a):
         do("v", "transpose", out, a)
 
-    def total_of(out, a):
-        do("v", "tensor_reduce", out, a, AxisListType.X, A.add)
-
     def quant(name, a, b, tile, lo):
         do("v", "quantize_mx", codes(name, a, b), plane(name, a, b), v2(tile, lo, lo + 4 * (b - a)), outs=2)
 
-    def mm(bank, n, l, la, r, ra, start=True, stop=True):
+    def mm(bank, n, l, la, r, ra):
         do("p", "matmul_mx", v2("ps%d" % bank, 0, n), codes(l, la, la + 128), plane(l, la, la + 128),
-           codes(r, ra, ra + n), plane(r, ra, ra + n), start, stop)
+           codes(r, ra, ra + n), plane(r, ra, ra + n), True, True)
 
     def iota(out, pattern, base, cm, flag=True):
         if flag:
@@ -198,7 +199,8 @@ def rank_program(g, core, T, topo):
 
     off = [r for r in range(N) if r != rank and topo.chip(T.cores[r]) != topo.chip(core)]
     near = [r for r in range(N) if r != rank and topo.chip(T.cores[r]) == topo.chip(core)]
-    perm = off + near + [rank]
+    perm = off + sorted(near + [rank])
+    kn, ko = perm.index(near[0]), perm.index(rank)
     share = {r: 8 if r in near else 4 for r in off + near}
     every = sum(share.values())
     used, mask = [], {}
@@ -208,23 +210,21 @@ def rank_program(g, core, T, topo):
         mask[r] = sum(1 << e for e in es)
     sent = [0]
 
-    def send(ks, sem, pairs):
+    def send(sem, trio):
         trs = []
-        for k, (src, dst) in zip(ks, pairs):
+        for r, src, dst in trio:
             touch("g", src[1], [])
-            rid, pid = topo.addr(T.cores[perm[k]])[:2]
-            trs.append(RemoteDMATransfer(dst_ids=[DstId(rid=rid, pnc=pid)], dma_engine_mask=mask[perm[k]],
+            rid, pid = topo.addr(T.cores[r])[:2]
+            trs.append(RemoteDMATransfer(dst_ids=[DstId(rid=rid, pnc=pid)], dma_engine_mask=mask[r],
                                          remote_sem=T.sem[sem], src=src[0], dst=dst[0]))
-            sent[0] += share[perm[k]]
+            sent[0] += share[r]
         g.remote_dma_fused(trs, local_sem=T.sem.sent)
 
-    def send_cols(ks, sem, sem2, slot, land):
+    def send_cols(rs, lo, sem, sem2, slot, land):
         u8 = dt.uint8
-        send(ks, sem, [(codes(slot, 128 * k, 128 * k + 128, u8), codes(land, 128 * rank, 128 * rank + 128, u8)) for k in ks])
-        send(ks, sem2, [(plane(slot, 128 * k, 128 * k + 128), plane(land, 128 * rank, 128 * rank + 128)) for k in ks])
-
-    far_ks, near_ks = list(range(len(off))), list(range(len(off), N - 1))
-    all_ks = far_ks + near_ks
+        at = [(r, lo + 128 * k) for k, r in enumerate(rs)]
+        send(sem, [(r, codes(slot, c, c + 128, u8), codes(land, 128 * rank, 128 * rank + 128, u8)) for r, c in at])
+        send(sem2, [(r, plane(slot, c, c + 128), plane(land, 128 * rank, 128 * rank + 128)) for r, c in at])
 
     dma("s", "lpl", v2("plb", 0, 8), ext(T.pl[:, 0:8]))
     dma("a", "lx0", v2("xb", 0, 512), ext(T.x[:, 0:512]))
@@ -234,160 +234,180 @@ def rank_program(g, core, T, topo):
     dma("s", "lwv", v2("wvb", 0, 2048), ext(T.wv[:]))
     dma("s", "lw", v2("wb", 0, 512), ext(T.w[:]))
 
+    up = 1 if rank == 0 else -1
     iota(one("pc"), [[0, 1]], 0, 1, False)
-    iota(v2("sa1", 0, 16), [[0, 4], [-2, 2], [0, 2]], 1, 0)
-    iota(v2("sa0", 0, 16), [[0, 8], [-2, 2]], 1, 0)
+    iota(v2("io4", 0, 4), [[1, 4]], 0, 0)
+    iota(one("p8"), [[0, 1]], 8, 1, False)
+    iota(v2("sgn", 0, 32), [[0, 32]], 1, 0)
     iota(v2("vb1", 0, 128), [[32, 8], [1, 16]], -128, 0)
     iota(v2("ctb", 0, 32), [[1, 4], [64, 8]], 0, 0)
     iota(v2("c8", 0, 32), [[0, 4], [1, 8]], 0, 0)
     iota(v2("q16", 0, 64), [[0, 4], [4, 16]], 0, 0)
-    iota(v2("nadd", 0, 32), [[256, 4], [0, 8]], 1, 0)
-    iota(v2("sb0", 0, 32), [[0, 16], [-2, 2]], 1, 0)
-    iota(v2("sb1", 0, 32), [[0, 8], [-2, 2], [0, 2]], 1, 0)
-    iota(v2("hm", 0, 32), [[0, 4], [-1, 2], [0, 4]], 1, 0)
-    iota(v2("c64", 0, 16), [[64, 16]], -1024, 0)
+    iota(v2("iof", 0, 128), [[up, 128]], START[rank], 0)
+    for h in range(2):
+        iota(half("plc", h), [[32, 8], [1, 16]], 256 * h - 256, 0)
 
-    fill(v2("zt", 0, 576), 0.0)
+    def bits(n, sh, m, src="pc"):
+        ts(one(n), one(src), sh, A.arith_shift_right, m, A.bitwise_and)
+
+    fill(v2("zt", 0, 512), 0.0)
+    bits("m4", 0, 3)
+    bits("pos", 3, 3)
     fill(v2("w1t", 512, 1024), 0.0)
-    for n, sh in (("b4", 4), ("b3", 3)):
-        ts(one(n), one("pc"), sh, A.arith_shift_right, 1, A.bitwise_and)
-    ts(one("t1a"), one("b4"), TINY, A.mult)
-    ts(one("t0a"), one("b3"), TINY, A.mult)
+    ts(one("c0"), one("m4"), 2.0, A.not_equal, 4.0, A.mult)
+    ts(one("c1"), one("m4"), 2.0, A.is_equal, 4.0, A.mult)
+    bits("b4", 4, 1)
+    fill(v2("sgn", 3, 16, 4), -1.0)
+    ts(v2("offg", 0, 8, 2), v2("io4", 0, 4), one("c0"), A.add)
+    ts(v2("offg", 1, 8, 2), v2("io4", 0, 4), one("c1"), A.add)
+    bits("r2", 2, 7, "p8")
+    ts(one("nz"), one("pos"), 0.5, A.is_lt, -1.0, A.add)
+    ts(one("k0"), one("pos"), 1.0, A.max, -256.0, A.mult)
+    ts(one("tp"), one("r2"), 2.5, A.is_lt, TINY, A.mult)
     ts(one("h16"), one("b4"), 16.0, A.mult)
+    ts(one("kg"), one("nz"), 0.5, A.add, HIGH, A.mult)
+    ts(one("kk"), one("k0"), 1024.0, A.add)
     quant("xq", 256, 384, "zt", 0)
-    fill(v2("a1", 0, 32), 0.25)
-    fill(v2("a1", 0, 32, 4), LOW)
 
-    def plane_cols(k, b, t):
-        return v2("w1t", 512 * b + t, 512 * b + 512, 32) if k == 1 else v2("w2t", 576 * b + 64 + t, 576 * b + 564, 16)
+    def planes(tile, src, t):
+        tt(v2(tile, 16 + t, 1024, 32), by(v2(src, 0, 8), v2("offg", 2 * t, 2 * t + 2)), v2("sgn", 0, 32), A.mult)
+
+    def blank(win, c):
+        for a, b in ((896, 1153), (1281, 1409), (1537, 1665)):
+            act(v2(win, a, b), v2("zt", 0, b - a), ACT.Identity, bias=c)
 
     act(v2("w1t", 0, 512), v2("zt", 0, 512), ACT.Copy)
-    act(v2("p1f", 0, 8), v2("plb", 0, 8), ACT.Copy)
-    for t in range(4):
-        act(plane_cols(1, 0, t), v2("sa0", 0, 16), ACT.Copy, scale=v2("p1f", t, t + 1))
+    act(v2("n1", 256, 288), v2("zt", 0, 32), ACT.Copy)
+    act(v2("d1", 256, 288), v2("zt", 0, 32), ACT.Copy)
+    act(v2("d1", 0, 256), v2("zt", 0, 256), ACT.Identity, bias=one("nz"))
     act(v2("val1", 0, 128), v2("vb1", 0, 128), ACT.Identity, bias=one("h16"))
-    act(v2("win1", LIST1, LIST1 + 516), v2("zt", 0, 516), ACT.Identity, bias=128.0)
+    blank("win1", 128.0)
+    act(v2("f8", 0, 32), v2("c8", 0, 32), ACT.Sign)
     for b in range(2):
-        act(v2("w2t", 576 * b, 576 * b + 576), v2("zt", 0, 576), ACT.Copy)
-    act(v2("ind2", 256, 416), v2("zt", 0, 160), ACT.Copy)
-    act(v2("am", 0, 288), v2("zt", 0, 288), ACT.Identity, bias=1.0)
-    act(v2("a2", 0, 64), v2("zt", 0, 64), ACT.Identity, bias=0.25)
+        act(v2("w2t", 512 * b, 512 * b + 512), v2("zt", 0, 512), ACT.Copy)
     for t in range(4):
-        ts(plane_cols(1, 1, t), v2("sa1", 0, 16), v2("plb", 4 + t, 5 + t), A.mult)
+        planes("w1t", "plb", t)
 
-    quant("w1", 128, 256, "w1t", 512)
     quant("xq", 0, 128, "xb", 0)
     quant("w1", 0, 128, "w1t", 0)
+    quant("w1", 128, 256, "w1t", 512)
     quant("xq", 128, 256, "xb", 512)
     for h in range(2):
-        for b in (1, 0):
+        for b in range(2):
             mm(2 * h + b, 128, "w1", 128 * b, "xq", 128 * h)
-    prod = lambda h, b: v2("ps%d" % (2 * h + b), 0, 128)
 
-    def gate(k, h):
-        o = half("g%d" % k, h)
-        if k == 1:
-            ts(o, prod(h, 1), one("t1a"), A.is_ge, LOW, A.mult)
-        else:
-            tt(o, prod(h, 1), half("tb2", h), A.is_ge)
+    def gate(k, a, n, bank):
+        ts(v2("g%d" % k, a, a + n), v2("ps%d" % bank, 0, n), one("tp"), A.is_lt, one("kg"), A.mult)
 
-    def bound(k, h):
-        o = half("g%d" % k, h)
-        if k == 1:
-            ts(o, o, one("t0a"), A.add)
-        else:
-            ts(o, o, LOW, A.mult, one("t0b"), A.add)
+    def apart(k, a, n, bank):
+        tt(v2("n%d" % k, a, a + n), v2("ps%d" % bank, 0, n), v2("g%d" % k, a, a + n), A.is_ge)
 
-    def member(k, h):
-        tt(half("ind%d" % k, h), prod(h, 0), half("g%d" % k, h), A.is_lt)
+    gate(1, 0, 128, 0)
+    gate(1, 128, 128, 2)
+    apart(1, 0, 128, 1)
+    apart(1, 128, 128, 3)
+    turn32(half("tn1", 0), half("n1", 0))
+    scan(v2("v1", 0, 288), v2("n1", 0, 288), v2("d1", 0, 288), one("kk"), A.add, A.add)
+    turn32(half("tn1", 1), half("n1", 1))
+    turn32(v2("tv1", 0, 288), v2("v1", 0, 288))
+    scan(v2("r1", 0, 32), v2("tn1", 4, 256, 8), v2("tv1", 4, 256, 8), 0.0, A.mult, A.max)
+    bits("r8", 2, 7)
+    ts(v2("do1", 0, 8), v2("r1", 3, 32, 4), -1.0, A.mult, float(TOP), A.add)
+    cp(by(v2("win1", 0, 1808), v2("do1", 0, 8)), v2("val1", 0, 128))
 
-    def count1(h):
-        scan(half("C1", h), half("ind1", h), v2("zt", 0, 128), v2("C1", 127, 128) if h else 0.0, A.add, A.add)
+    def listed(win, d):
+        if d == 0:
+            return (T[win][:, 1023:895:-1], [(win, 896, 1024, 1, 1)], [])
+        return v2(win, 256 * d + 769, 256 * d + 897)
 
-    gate(1, 0)
-    bound(1, 0)
-    gate(1, 1)
-    member(1, 0)
-    bound(1, 1)
-    count1(0)
-    member(1, 1)
-    turn32(half("tI1", 0), half("ind1", 0))
-    count1(1)
-    turn32(half("tC1", 0), half("C1", 0))
-    turn32(half("tI1", 1), half("ind1", 1))
-    turn32(half("tC1", 1), half("C1", 1))
-    tt(v2("M1", 0, 32), v2("tI1", 0, 256, 8), v2("tC1", 0, 256, 8), A.mult)
-    scan(v2("R1", 0, 32), v2("a1", 0, 32), v2("M1", 0, 32), 0.0, A.add, A.max)
-    ts(v2("do1", 0, 8), v2("R1", 3, 32, 4), 4.0, A.mult)
-    cp(by(v2("win1", 0, 1040), v2("do1", 0, 8)), v2("val1", 0, 128))
-
-    def spread(win, lo, wd):
+    def spread(win, wd):
         for k in range(4):
             for h in range(2):
-                o, z = v3(wd, 8 * k, 8 * k + 8, 16 * h, 16 * h + 16), v2(win, lo + perm[k], lo + perm[k] + 509, 4)
+                o, z = v3(wd, 8 * k, 8 * k + 8, 16 * h, 16 * h + 16), listed(win, perm[k])
                 if k > 1 or k + h == 0:
                     act(o, z, ACT.Copy)
                 else:
                     cp(o, z)
 
-    def pick(dst, a, b, src, w, offs, k):
+    def pick(dst, a, b, src, w, offs, k, part="cs"):
         o = v2(offs, 8 * k, 8 * k + (b - a) // 16)
-        cp(codes(dst, a, b, dt.uint32), by(codes(src, 0, w, dt.uint32), o))
-        act(plane(dst, a, b), by(plane(src, 0, w), o), ACT.Copy)
+        if "c" in part:
+            cp(codes(dst, a, b, dt.uint32), by(codes(src, 0, w, dt.uint32), o))
+        if "s" in part:
+            act(plane(dst, a, b), by(plane(src, 0, w), o), ACT.Copy)
 
-    spread("win1", LIST1, "wd1")
+    spread("win1", "wd1")
     for hf in range(2):
         a, b = 16 * hf, 16 * hf + 16
         turn32(v3("t21", a, b, 0, 32), v3("wd1", a, b, 0, 32))
+        if hf == 1:
+            bits("gi", 4, 7)
         tt(v2("l1", a, b), v3i("t21", a, b, 0), v3i("t21", a, b, 16), A.add)
+        if hf == 1:
+            cp(one("gf"), one("gi"))
         cp(v2("off1", a, b), v2("l1", a, b))
         if hf == 0:
             pick("slota", 0, 256, "xq", 384, "off1", 0)
+            send_cols(off, 0, "c1", "c1", "slota", "landa")
         else:
-            pick("slota", 256, 384, "xq", 384, "off1", 2)
-        send_cols(far_ks if hf == 0 else near_ks, "c1", "c1", "slota", "landa")
-    send(all_ks, "n1", [(v2("off1", 8 * k, 8 * k + 8), v2("nl", 8 * rank, 8 * rank + 8)) for k in all_ks])
-    pick("landa", 128 * rank, 128 * rank + 128, "xq", 384, "off1", 3)
-    cp(v2("nl", 8 * rank, 8 * rank + 8), v2("off1", 24, 32))
+            ts(v2("dm1", 0, 32), v2("c8", 0, 32), one("gf"), A.is_equal)
+            pick("slota", 256, 384, "xq", 384, "off1", kn)
+            send_cols(near, 256, "c1", "c1", "slota", "landa")
 
-    for h in range(2):
-        iota(half("plc", h), [[32, 4], [256, 2], [1, 16]], 128 * h - 256, 0)
-    iota(v2("io2", 0, 128), [[2, 128]], 0, 0)
-    iota(v2("win2", LIST2, LIST2 + 512), [[0, 512]], 256, 0)
-    for n, sh, m in (("b2", 2, 1), ("qi", 0, 15), ("gi", 4, 7)):
-        ts(one(n), one("pc"), sh, A.arith_shift_right, m, A.bitwise_and)
-    for b in range(2):
-        tt(v2("sb%d" % b, 0, 32), v2("sb%d" % b, 0, 32), v2("hm", 0, 32), A.mult)
+    def ends(a, b):
+        return v2("tv1", 260 + 8 * a, 253 + 8 * b, 8)
+
+    tt(v2("pd1", 0, 32), v2("l1", 0, 32), v2("dm1", 0, 32), A.mult)
+    ts(one("mf"), one("r8"), 1.0, A.is_equal)
+    ts(v2("ea", 0, 1), ends(0, 1), -1.0, A.mult, START[0] + 128.0, A.add)
+    scan(v2("pe1", 0, 32), v2("f8", 0, 32), v2("pd1", 0, 32), 0.0, A.mult, A.add)
+    for d in range(1, 4):
+        ts(v2("ea", d, d + 1), ends(d, d + 1), 128.0 - START[d], A.add)
+    for k in (0, 2):
+        ts(v2("msg", 4 * perm[k], 4 * perm[k + 1] + 1, 4 * (perm[k + 1] - perm[k])), v2("pe1", 8 * k + 7, 8 * k + 16, 8),
+           256.0 * rank, A.add)
+    ts(v2("eb", 0, 4), v2("ea", 0, 4), 0.0, A.max, one("mf"), A.mult)
+    ts(v2("msg", 1, 16, 4), ends(0, 4), one("mf"), A.mult)
+    bits("qi", 0, 15)
+    ts(v2("ec", 0, 4), v2("eb", 0, 4), 1.0, A.min, JUMP[rank], A.mult)
+    bits("b2", 2, 1)
     ts(one("q4"), one("qi"), 4.0, A.mult)
-    ts(one("t0b"), one("b2"), TINY, A.mult)
-    cp(one("gf"), one("gi"))
-    ts(v2("am", 128, 129), one("b4"), -1.0, A.mult, 1.0, A.add)
-    fill(v2("a2", 0, 64, 4), LOW)
+    tt(v2("msg", 2, 16, 4), v2("eb", 0, 4), v2("ec", 0, 4), A.add)
+    send("m1", [(r, v2("msg", 4 * r, 4 * r + 3), v2("nl", 4 * rank, 4 * rank + 3)) for r in off + near])
+    pick("landa", 128 * rank, 128 * rank + 128, "xq", 384, "off1", ko)
+    cp(v2("nl", 4 * rank, 4 * rank + 3), v2("msg", 4 * rank, 4 * rank + 3))
+
+    def filled(s):
+        ts(half("d2", s), v2("io2", 0, 128), v2("nl", 4 * s + 1, 4 * s + 2), A.is_equal, one("j%d" % (s == 1)), A.mult)
+
+    def to_row(s):
+        dma("s", "tb%d" % s, (T.tabrow[0:1, 128 * s:128 * s + 128], half("tabrow", s)[1], []), v2("nl", 4 * s, 4 * s + 1))
+
+    to_row(rank)
+    cp(one("bf"), one("b2"))
+    for k in range(2):
+        ts(one("j%d" % k), one("mf"), JUMP[k], A.mult, one("nz"), A.add)
+    fill(v2("tabrow", 512, 520), -1.0)
+    ts(one("k2"), one("kk"), one("bf"), A.mult)
     ts(v2("offct", 0, 32), v2("ctb", 0, 32), one("q4"), A.add)
-    act(v2("p2f", 0, 8), v2("p2b", 0, 8), ACT.Copy)
-    for b in range(2):
-        for t in range(4):
-            act(plane_cols(2, b, t), v2("sb%d" % b, 0, 32), ACT.Copy, scale=v2("p2f", 4 * b + t, 4 * b + t + 1))
-    act(v2("X", 0, 64), v2("zt", 0, 64), ACT.Identity, bias=8.0)
-    act(v2("f8", 0, 32), v2("c8", 0, 32), ACT.Sign)
-    act(v2("f16", 0, 64), v2("q16", 0, 64), ACT.Sign)
-    act(v2("tabrow", 512, 520), v2("zt", 0, 8), ACT.Copy)
-    act(v2("idp", 0, 32), v2("zt", 0, 32), ACT.Copy)
-    act(v2("val2", 0, 256), v2("plc", 0, 256), ACT.Identity, bias=one("h16"))
+    ts(v2("io2", 0, 128), v2("iof", 0, 128), one("mf"), A.mult)
+    ts(one("lo"), one("k2"), -128.0, A.add)
+    for t in range(4):
+        planes("w2t", "p2b", t)
     quant("wvq", 0, 512, "wvb", 0)
-    quant("w2", 0, 144, "w2t", 0)
-    quant("w2", 144, 288, "w2t", 576)
+    quant("w2", 0, 256, "w2t", 0)
     quant("hq", 512, 640, "zt", 0)
-    ts(v2("dmp", 0, 16), v2("c64", 0, 16), one("q4"), A.add, 0.0625, A.mult)
-    ts(v2("dm1", 0, 32), v2("c8", 0, 32), one("gf"), A.is_equal)
+    quant("wq", 0, 128, "wb", 0)
+    filled(rank)
     ts(v2("dm2", 0, 64), v2("q16", 0, 64), one("q4"), A.is_equal)
+    act(v2("f16", 0, 64), v2("q16", 0, 64), ACT.Sign)
+    act(v2("val2", 0, 256), v2("plc", 0, 256), ACT.Identity, bias=one("h16"))
+    blank("win2", 256.0)
 
     for s in range(N):
         if s != rank:
             arrive("c1", 2 * every, codes("landa", 128 * s, 128 * s + 128), plane("landa", 128 * s, 128 * s + 128))
-            arrive("n1", every, v2("nl", 8 * s, 8 * s + 8))
-    for t in range(4):
-        pick("ct", 128 * t, 128 * t + 128, "landa", 512, "offct", t)
+            arrive("m1", every, v2("nl", 4 * s, 4 * s + 3))
 
     def empty(q, tile, lo, t, bank, n, f):
         o, z = v2(tile, lo + t, lo + 4 * n, 4), v2("ps%d" % bank, 0, n)
@@ -398,125 +418,154 @@ def rank_program(g, core, T, topo):
         else:
             act(o, z, ACT.Copy, scale=0.0625) if q == "a" else ts(o, z, 0.0625, A.mult)
 
-    for t in range(4):
-        mm(t, 512, "ct", 128 * t, "wvq", 0)
-        empty("avav"[t], "vt", 0, t, t, 512, "copy")
-        if t == 1:
-            ts(v2("fF", 0, 32), v2("nl", 0, 32), 255.5, A.is_lt)
-            cp(v2("nf", 0, 32), v2("nl", 0, 32))
-            for m in range(4):
-                x = 32 * (m % 2) + 12 + 16 * (m // 2)
-                total_of(v2("X", x, x + 1), v2("fF", 8 * m, 8 * m + 8))
-            tt(v2("nt", 0, 32), v2("nf", 0, 32), v2("nadd", 0, 32), A.add)
-            turn32(v2("ntt", 0, 32), v2("nt", 0, 32))
-    dma("s", "ltb", (T.tabrow[0:1, 0:512], v2("tabrow", 0, 512)[1], []), (T.ntt[0:32, 0:16], v2("ntt", 0, 32)[1], []))
-    do("g", "partition_broadcast", v2("tab", 0, 520), (T.tabrow[0:1, 0:520], v2("tabrow", 0, 520)[1], []), 128)
-    quant("vq", 0, 512, "vt", 0)
-    for h, who in enumerate(("aaaa", "aaav")):
-        for t in range(4):
-            bank = 4 * (1 - h) + t
-            mm(bank, 256, "ct", 128 * t, "landa", 256 * h)
-            empty(who[t], "at", 1024 * h, t, bank, 256, "relu")
-        quant("aq", 256 * h, 256 * h + 256, "at", 1024 * h)
-    for lo, n, b0, who in ((0, 256, 4, "aava"), (256, 128, 0, "aaaa"), (384, 128, 4, "avav")):
-        for i in range(4):
-            mm(b0 + i, n, "vq", 128 * i, "aq", lo)
-        if lo == 384:
-            for b in (1, 0):
-                mm(b, 128, "w2", 144 * b + 16, "hq", 0, True, False)
-                mm(b, 128, "w2", 144 * b, "hq", 256, False, True)
-            for b in (1, 0):
-                mm(2 + b, 128, "w2", 144 * b + 16, "hq", 128, True, False)
-        for i in range(4):
-            empty(who[i], "ht", 4 * lo, i, b0 + i, n, "scale")
-        if lo == 0:
-            turn32(v2("xt", 0, 64), v2("X", 0, 64))
-            for h in range(2):
-                total_of(one("cnt%d" % h), v2("xt", 32 * h, 32 * h + 32))
-        quant("hq", lo, lo + n, "ht", 4 * lo)
-        if lo == 0:
-            for h in range(2):
-                ts(half("tb2", h), v2("io2", 0, 128), one("cnt%d" % h), A.is_lt, one("t0a"), A.mult)
-    for b in (1, 0):
-        mm(2 + b, 128, "w2", 144 * b, "hq", 384, False, True)
+    runs = ((0, 256), (256, 128), (384, 128))
+    free, held = list(range(8)), {}
 
-    def sign(h):
-        act(half("J2", h), half("ind2", h), ACT.Identity, scale=2 * FAR, bias=-FAR)
+    def take(key):
+        held[key] = free.pop(0)
+        return held[key]
 
-    gate(2, 0)
-    bound(2, 0)
-    gate(2, 1)
-    member(2, 0)
-    sign(0)
-    bound(2, 1)
-    scan(v2("C2", 0, 128), v2("am", 0, 128), v2("ind2", 0, 128), 0.0, A.mult, A.add)
-    member(2, 1)
-    sign(1)
-    turn32(v2("tC2", 0, 128), v2("C2", 0, 128))
-    scan(v2("C2", 128, 416), v2("am", 0, 288), v2("ind2", 128, 416), v2("C2", 127, 128), A.mult, A.add)
-    turn32(half("tJ2", 0), half("J2", 0))
-    turn32(half("tJ2", 1), half("J2", 1))
-    turn32(v2("tC2", 128, 416), v2("C2", 128, 416))
-    for h in range(2):
-        tt(v2("D2", 32 * h, 32 * h + 32), v2("tC2", 128 * h, 128 * h + 128, 4), v2("tC2", 272, 400, 4), A.add)
-    tt(v2("M2", 0, 64), v2("D2", 0, 64), v2("tJ2", 0, 256, 4), A.min)
-    scan(v2("R2", 0, 64), v2("a2", 0, 64), v2("M2", 0, 64), 0.0, A.add, A.max)
-    tt(v2("dst2", 0, 16), v2("R2", 3, 64, 4), v2("dmp", 0, 16), A.max)
-    ts(v2("do2", 0, 16), v2("dst2", 0, 16), 4.0, A.mult, 256.0, A.add)
-    cp(by(v2("win2", 0, 2320), v2("do2", 0, 16)), v2("val2", 0, 256))
-    spread("win2", LIST2, "wd2")
-    for hf in range(2):
-        a, b = 16 * hf, 16 * hf + 16
-        turn32(v3("t22", a, b, 0, 32), v3("wd2", a, b, 0, 32))
-        tt(v2("l2", a, b), v3i("t22", a, b, 0), v3i("t22", a, b, 16), A.add)
-        cp(v2("off2", a, b), v2("l2", a, b))
-        if hf == 0:
-            pick("slotb", 0, 256, "hq", 640, "off2", 0)
+    def drop(key):
+        free.append(held[key])
+        return held[key]
+
+    for w in PLAN:
+        c, z = w[:2], w[2:]
+        if w[0] == "p":
+            pick("ct", 128 * int(z[0]), 128 * int(z[1]) + 128, "landa", 512, "offct", int(z[0]), w[1])
+        elif c == "mV":
+            mm(take(w[1:]), 512, "ct", 128 * int(z), "wvq", 0)
+        elif c == "eV":
+            empty(w[-1], "vt", 0, int(z[0]), drop(w[1:3]), 512, "copy")
+        elif c == "mA":
+            mm(take(w[1:]), 256, "ct", 128 * int(z[1]), "landa", 256 * int(z[0]))
+        elif c == "eA":
+            empty(w[-1], "at", 1024 * int(z[0]), int(z[1]), drop(w[1:-1]), 256, "relu")
+        elif c == "mH":
+            mm(take(w[1:]), runs[int(z[0])][1], "vq", 128 * int(z[1]), "aq", runs[int(z[0])][0])
+        elif c == "eH":
+            empty(w[-1], "ht", 4 * runs[int(z[0])][0], int(z[1]), drop(w[1:-1]), runs[int(z[0])][1], "scale")
+        elif c == "qv":
+            quant("vq", 0, 512, "vt", 0)
+        elif c == "qa":
+            quant("aq", 256 * int(z), 256 * int(z) + 256, "at", 1024 * int(z))
+        elif c == "fa":
+            if int(z) != rank:
+                filled(int(z))
+        elif c == "cR":
+            s = int(z)
+            ts(one("in%d" % s), v2("v2", 128 * s - 1, 128 * s), v2("nl", 4 * s - 2, 4 * s - 1), A.subtract, one("lo"), A.max)
+        elif c == "sR":
+            s = int(z)
+            scan(half("v2", s), half("n2", s), half("d2", s), one("in%d" % s if s else "k2"), A.add, A.add)
+        elif w == "tab":
+            for s in off + near:
+                to_row(s)
+            do("g", "partition_broadcast", v2("tab", 0, 520), (T.tabrow[0:1, 0:520], v2("tabrow", 0, 520)[1], []), 128)
         else:
-            tt(v2("pd", 0, 32), v2("l2", 0, 32), v2("dm1", 0, 32), A.mult)
-            pick("slotb", 256, 384, "hq", 640, "off2", 2)
-        send_cols(far_ks if hf == 0 else near_ks, "c2_%d" % rank, "s2_%d" % rank, "slotb", "landb")
-    scan(v2("pds", 0, 32), v2("f8", 0, 32), v2("pd", 0, 32), 0.0, A.mult, A.add)
-    cp(v2("offD", 0, 4), v2("pds", 7, 32, 8))
-    tt(v2("gm", 0, 64), by(v2("tab", 0, 520), v2("offD", 0, 4)), v2("dm2", 0, 64), A.mult)
-    scan(v2("gms", 0, 64), v2("f16", 0, 64), v2("gm", 0, 64), 0.0, A.mult, A.add)
-    cp(v2("idu", 0, 4), v2("gms", 15, 64, 16))
-    send(all_ks, "n2", [(v2("idu", k, k + 1), v2("idl", 8 * rank, 8 * rank + 1)) for k in all_ks])
-    pick("landb", 128 * rank, 128 * rank + 128, "hq", 640, "off2", 3)
-    cp(v2("idl", 8 * rank, 8 * rank + 1), v2("idu", 3, 4))
-    quant("wq", 0, 128, "wb", 0)
+            j = int(z[-1])
+            lo, n = runs[j]
+            a, b = lo // 32, (lo + n) // 32
+            if c == "qh":
+                quant("hq", lo, lo + n, "ht", 4 * lo)
+            elif c == "mR":
+                mm(take(w[1:]), n, "w2", 128 * "ab".index(z[0]), "hq", lo)
+            elif c == "gR":
+                gate(2, lo, n, drop("Ra%d" % j))
+            elif c == "nR":
+                apart(2, lo, n, drop("Rb%d" % j))
+            elif c == "tn":
+                turn32(v2("tn2", lo, lo + n), v2("n2", lo, lo + n))
+            elif c == "tv":
+                turn32(v2("tv2", lo, lo + n), v2("v2", lo, lo + n))
+            elif c == "uR":
+                scan(v2("r2", 8 * a, 8 * b), v2("tn2", lo, lo + n, 4), v2("tv2", lo, lo + n, 4), 0.0, A.mult, A.max)
+            elif c == "dR":
+                ts(v2("do2", a, b), v2("r2", 8 * a + 7, 8 * b, 8), -1.0, A.mult, float(TOP), A.add)
+            else:
+                cp(by(v2("win2", 0, 1808), v2("do2", a, b)), v2("val2", 16 * a, 16 * b))
+
+    def numbers(a, b, step):
+        if step == 0:
+            tt(v2("pd", 8 * a, 8 * b), v2("l2", 8 * a, 8 * b), v2("dm1", 8 * a, 8 * b), A.mult)
+        elif step == 1:
+            scan(v2("pds", 8 * a, 8 * b), v2("f8", 8 * a, 8 * b), v2("pd", 8 * a, 8 * b), 0.0, A.mult, A.add)
+        elif step == 2:
+            cp(v2("offD", a, b), v2("pds", 8 * a + 7, 8 * b, 8))
+        elif step == 3:
+            tt(v2("gm", 16 * a, 16 * b), by(v2("tab", 0, 520), v2("offD", a, b)), v2("dm2", 16 * a, 16 * b), A.mult)
+        else:
+            scan(v2("gms", 16 * a, 16 * b), v2("f16", 16 * a, 16 * b), v2("gm", 16 * a, 16 * b), 0.0, A.mult, A.add)
+
+    def slot_of(s):
+        return (T.idd[s], [("idd", s, s + 1, 1, 1)], [])
+
+    def send_numbers(rs):
+        send("m2", [(r, v2("gms", 16 * perm.index(r) + 15, 16 * perm.index(r) + 16), slot_of(rank)) for r in rs])
+
+    spread("win2", "wd2")
+    turn32(v3("t22", 0, 16, 0, 32), v3("wd2", 0, 16, 0, 32))
+    tt(v2("l2", 0, 16), v3i("t22", 0, 16, 0), v3i("t22", 0, 16, 16), A.add)
+    cp(v2("off2", 0, 16), v2("l2", 0, 16))
+    numbers(0, 2, 0)
+    pick("slotb", 0, 256, "hq", 640, "off2", 0)
+    send_cols(off, 0, "c2_%d" % rank, "s2_%d" % rank, "slotb", "landb")
+    numbers(0, 2, 1)
+    turn32(v3("t22", 16, 32, 0, 32), v3("wd2", 16, 32, 0, 32))
+    numbers(0, 2, 2)
+    tt(v2("l2", 16, 32), v3i("t22", 16, 32, 0), v3i("t22", 16, 32, 16), A.add)
+    numbers(0, 2, 3)
+    cp(v2("off2", 16, 32), v2("l2", 16, 32))
+    numbers(0, 2, 4)
+    numbers(2, 4, 0)
+    send_numbers(off)
+    pick("slotb", 256, 384, "hq", 640, "off2", kn)
+    send_cols(near, 256, "c2_%d" % rank, "s2_%d" % rank, "slotb", "landb")
+    numbers(2, 4, 1)
+    pick("landb", 128 * rank, 128 * rank + 128, "hq", 640, "off2", ko)
+    for step in range(2, 5):
+        numbers(2, 4, step)
+    send_numbers(near)
 
     for s in range(N):
         if s != rank:
             arrive("c2_%d" % s, share[s], codes("landb", 128 * s, 128 * s + 128))
             arrive("s2_%d" % s, share[s], plane("landb", 128 * s, 128 * s + 128))
-            arrive("n2", every, v2("idl", 8 * s, 8 * s + 1))
-    turn = [rank] + near + off
+            arrive("m2", every, slot_of(s))
 
     def store_codes(q, s):
         dma(q, "oc%d" % s, ext(T.oc[:, 512 * s:512 * s + 512]), codes("landb", 128 * s, 128 * s + 128, dt.uint8))
 
-    for s in [rank] + off:
-        store_codes("s", s)
-    for i, s in enumerate(turn):
-        if s in near:
-            store_codes("a", s)
-        bank = (6, 7, 2, 3)[i]
+    def product(q, s, bank):
         mm(bank, 128, "wq", 0, "landb", 128 * s)
         o, z = v2("yb", 128 * s, 128 * s + 128), v2("ps%d" % bank, 0, 128)
-        if i < 3:
-            act(o, z, ACT.Copy)
-        else:
-            cp(o, z)
-        dma("a" if i < 3 else "s", "yy%d" % s, ext(T.y[:, 128 * s:128 * s + 128]), o)
+        act(o, z, ACT.Copy) if q == "a" else cp(o, z)
+
+    def store_y(q, s):
+        dma(q, "yy%d" % s, ext(T.y[:, 128 * s:128 * s + 128]), half("yb", s))
+
+    def store_id(q, s):
+        src = v2("gms", 16 * ko + 15, 16 * ko + 16) if s == rank else (T.idd[s, :, 0], slot_of(s)[1], [])
+        dma(q, "ii%d" % s, ext(T["id"][0:1, 128 * s:128 * s + 128]), src)
+
+    store_codes("s", rank)
+    product("a", rank, free[0])
+    store_y("a", rank)
+    store_id("s", rank)
+    for s in off:
+        store_codes("s", s)
+    store_codes("a", near[0])
+    product("a", near[0], free[1])
+    store_y("a", near[0])
+    product("a", off[0], free[2])
+    product("v", off[1], free[3])
     for k in range(4):
-        dma("a" if k % 2 else "s", "os%d" % k, ext(T.osc[4 * k:4 * k + 4, :]),
+        dma("s", "os%d" % k, ext(T.osc[4 * k:4 * k + 4, :]),
             (T.landbs[32 * k:32 * k + 4, 0:512], plane("landb", 0, 512)[1], []))
-    ts(v2("idp", 0, 4), v2("idl", 0, 32, 8), -1.0, A.add)
-    turn32(v2("idt", 0, 32), v2("idp", 0, 32))
-    for s in range(N):
-        dma("a" if s % 2 else "s", "ii%d" % s, ext(T["id"][0:1, 128 * s:128 * s + 128]),
-            (T.idt[s:128:32, 0:32], v2("idt", 0, 32)[1], []))
+    store_y("a", off[0])
+    store_y("s", off[1])
+    for i, s in enumerate(off + near):
+        store_id("as"[i % 2], s)
     total["sent"] = sent[0]
     for sem in SEMAPHORES:
         if total.get(sem, 0) > waited.get(sem, 0):

@@ -1,49 +1,51 @@
 from concourse.bass import DstId, RemoteDMATransfer
-from concourse.mybir import dt, AluOpType, AxisListType, ActivationFunctionType
+from concourse.mybir import dt, AluOpType, ActivationFunctionType
 
 F, B, I, U, H = "float32", "bfloat16", "int32", "uint16", "float16"
 Q, S8 = "float8_e4m3fn_x4", "uint8"
-COL = {n: ("ki", k) for k, n in enumerate(("pc", "pos", "b4", "m4", "qi", "gi", "p8", "r2", "r8", "b2"))}
-COL.update({n: ("kf", k) for k, n in enumerate(("tp", "nz", "kg", "k0", "kk", "lo", "h16", "c0", "c1", "q4", "gf", "mf",
-                                                "bf", "k2", "j0", "j1", "in1", "in2", "in3"))})
-SCRATCH = {"idd": ("dram", [4, 128, 1], F)}
+COL = {n: ("ki", k) for k, n in enumerate(("p2", "m4"))}
+COL.update({n: ("kf", k) for k, n in enumerate(("c0", "tp", "nz", "kg", "k0", "kk", "z1", "mf", "nb", "t2", "k2", "lo", "kh",
+                                                "bp", "j0", "j1", "sc", "cb", "in2"))})
+COL.update({n: ("kt", 32 * k) for k, n in enumerate(("pos", "h16", "q4", "bf", "g16"))})
+SCRATCH = {"ida": ("dram", [4, 128, 1], F), "idd": ("dram", [4, 128, 1], F)}
 for _n, _w, _t in (
         ("plb", 8, B), ("p2b", 8, B), ("xb", 1024, B), ("wvb", 2048, B), ("wb", 512, B),
-        ("w1t", 1024, B), ("zt", 512, B), ("w2t", 1024, B), ("at", 2048, B), ("vt", 2048, B), ("ht", 2048, B),
-        ("sgn", 32, B), ("val1", 128, B), ("val2", 256, B), ("win1", 1808, B), ("win2", 1808, B), ("ki", 16, I),
-        ("kf", 24, F), ("io4", 4, F), ("vb1", 128, F), ("ctb", 32, F), ("plc", 256, F), ("c8", 32, F), ("dm1", 32, F),
-        ("f8", 32, F), ("q16", 64, F), ("dm2", 64, F), ("f16", 64, F), ("iof", 128, F), ("io2", 128, H),
-        ("ea", 4, F), ("eb", 4, F), ("ec", 4, F), ("tabrow", 520, F), ("tab", 520, F), ("msg", 16, F), ("nl", 16, F),
+        ("wt", 528, B), ("zt", 512, B), ("at", 2048, B), ("vt", 2048, B), ("ht", 2048, B),
+        ("sgn", 32, B), ("val1", 128, B), ("val2", 256, B), ("win1", 1808, B), ("win2", 1808, B), ("ki", 4, I),
+        ("kf", 24, F), ("kr", 160, F), ("kt", 160, F), ("io8", 8, F), ("vb1", 128, F), ("ctb", 32, F), ("plc", 256, F),
+        ("c8", 32, F), ("dm1", 32, F), ("f8", 32, F), ("q16", 64, F), ("dm2", 64, F), ("f16", 64, F), ("iof", 128, F),
+        ("io2", 128, H), ("eb", 4, F), ("ec", 4, F), ("ed", 4, F), ("ee", 4, F), ("tabrow", 520, F), ("tab", 520, F),
+        ("ends", 4, F), ("msg", 4, F), ("nv", 16, F), ("sg", 512, B),
         ("g1", 256, B), ("n1", 288, B), ("d1", 288, B), ("v1", 288, H), ("tn1", 256, B), ("tv1", 288, H), ("r1", 32, F),
         ("l1", 32, F), ("l2", 32, F), ("pd1", 32, F), ("pe1", 32, F),
-        ("g2", 512, B), ("n2", 512, B), ("d2", 512, B), ("v2", 512, H), ("tn2", 512, B), ("tv2", 512, H), ("r2", 128, F),
+        ("g2", 512, B), ("n2", 512, B), ("d2", 512, H), ("v2", 512, H), ("tn2", 512, B), ("tv2", 512, H), ("r2", 128, F),
         ("pd", 32, F), ("pds", 32, F), ("gm", 64, F), ("gms", 64, F), ("yb", 512, F),
         ("offg", 8, U), ("do1", 8, U), ("do2", 16, U), ("off1", 32, U), ("off2", 32, U), ("offct", 32, U), ("offD", 4, U)):
     SCRATCH[_n] = ("sbuf", [128, _w], _t)
 for _n in ("wd1", "t21", "wd2", "t22"):
     SCRATCH[_n] = ("sbuf", [128, 32, 32], B)
-for _n, _w in (("w1", 256), ("xq", 384), ("slota", 384), ("landa", 512), ("ct", 512), ("wvq", 512), ("aq", 512), ("vq", 512),
-               ("w2", 256), ("hq", 640), ("slotb", 384), ("landb", 512), ("wq", 128)):
+for _n, _w in (("w1", 132), ("xq", 384), ("slota", 384), ("landa", 512), ("ct", 512), ("wvq", 512), ("aq", 512), ("vq", 512),
+               ("w2", 132), ("hq", 528), ("slotb", 384), ("landb", 512), ("wq", 128)):
     SCRATCH[_n + "c"] = ("sbuf", [128, _w], Q)
     SCRATCH[_n + "s"] = ("sbuf", [128, _w], S8)
 for _k in range(8):
     SCRATCH["ps%d" % _k] = ("psum", [128, 512], F)
 
-SEMAPHORES = (["sv", "sa", "sp", "sg", "sent", "c1", "m1", "m2", "lpl", "lx0", "lx1", "lp2", "lwv", "lw"]
+SEMAPHORES = (["sv", "sa", "sp", "sg", "sent", "c1", "s1", "m0", "m1", "m2", "lpl", "lx0", "lx1", "lp2", "lwv", "lw", "zc", "zs"]
               + ["%s_%d" % (n, k) for n in ("c2", "s2") for k in range(4)]
               + ["%s%d" % (n, k) for n in ("oc", "os", "yy", "ii", "tb") for k in range(4)])
 
 TINY = 2.0 ** -120
 HIGH = 2.0 ** 99
 TOP = 1792
-START = (768, 768, 512, 256)
-JUMP = (512.0, 640.0, 512.0, 512.0)
+START = (1152, 1152, 768, 384)
+JUMP = (384.0, 128.0)
 
-PLAN = ("pc00 ps00 pc33 mV0 pc22 ps33 mV3 ps22 pc11 ps11 mV2 mV1 eV00v eV30a mA00 eV20v mA01 mA03 mA02 eA00a eV10v mA10 "
-        "eA03a mA13 tab eA01v mA12 qv0 mA11 eA02a qa0 mH01 eA10a eA13a mH02 mH00 eA12v fa2 eA11a qa1 eH02v mH03 mH11 mH13 "
-        "eH01a mH12 eH00a eH03v eH13v eH11a qh0 mH10 mH21 eH12a fa0 eH10a mH23 mH22 fa1 eH21a mH20 qh1 fa3 eH23a eH20a "
-        "mRa0 eH22a mRa1 gR0 mRb0 mRb1 gR1 nR0 qh2 mRb2 sR0 mRa2 tn0 cR1 nR1 sR1 gR2 cR2 tv0 nR2 sR2 tn1 uR0 tn2 cR3 tv1 "
-        "dR0 sR3 uR1 xR0 tv2 dR1 uR2 xR1 dR2 xR2").split()
+PLAN = ("pc00 pc11 pc33 ps33v pc22 mV3 ps22a ps00a mV2 mA02 ps11a eV20a eV30v mV1 mV0 mA03 mA00 eV00a mA01 eA02v eV10v tab "
+        "eA03v mA10 eA00v eA01a mA11 mA12 mA13 qv1 eA10a qa0 mH03 qv0 mH02 eA12a eA11v mH12 mH00 eA13a mH01 eH12a eH03v "
+        "qa1 eH02v eH00a mH10 mH11 eH01a mH13 eH11v eH10v mH21 qh0 mH23 mH22 mH20 eH21v eH23v eH13a qh1 mH32 eH22a mH30 "
+        "eH32v eH20a mRa0 mH33 gR0v eH30a eH33a mH31 mRa1 mRb0 qh2 eH31a gR1v mRb1 nR0 qh3 sR0 nR1 mRa2 tv0 tn0 mRa3 gR2a "
+        "sR1 tn1 gR3v cR2 mRb2 mRb3 nR2 tv1 nR3 sR2 uR0 tn2 tn3 sR3 tv2 dR0 tv3 uR1 xR0 dR1 uR2 xR1 dR2 xR2").split()
 
 
 def rank_program(g, core, T, topo):
@@ -118,6 +120,9 @@ def rank_program(g, core, T, topo):
     def plane(name, a, b):
         return v2(name + "s", a, b)
 
+    def slot_of(name, s):
+        return (T[name][s], [(name, s, s + 1, 1, 1)], [])
+
     def by(win, off):
         return (win[0].indirect(off[0]), win[1], off[1])
 
@@ -174,6 +179,9 @@ def rank_program(g, core, T, topo):
 
     def act(out, a, f, **kw):
         do("a", "activation", out, a, f, **kw)
+
+    def lin(out, a, scale, bias, f=ACT.Identity):
+        act(out, a, f, scale=scale, bias=bias)
 
     def fill(out, c):
         do("v", "memset", out, c)
@@ -235,69 +243,73 @@ def rank_program(g, core, T, topo):
     dma("s", "lw", v2("wb", 0, 512), ext(T.w[:]))
 
     up = 1 if rank == 0 else -1
-    iota(one("pc"), [[0, 1]], 0, 1, False)
-    iota(v2("io4", 0, 4), [[1, 4]], 0, 0)
-    iota(one("p8"), [[0, 1]], 8, 1, False)
+    iota(one("p2"), [[0, 1]], 2, 2, False)
+    iota(v2("kr", 0, 32), [[1, 4], [0, 8]], 0, 0)
+    iota(v2("io8", 0, 8), [[1, 4], [0, 2]], 0, 0)
     iota(v2("sgn", 0, 32), [[0, 32]], 1, 0)
+    iota(v2("sgn", 6, 32, 8), [[0, 4]], -1, 0)
+    iota(v2("kr", 32, 64), [[16, 2], [0, 16]], 0, 0)
+    iota(v2("kr", 64, 96), [[0, 2], [4, 16]], 0, 0)
+    iota(v2("kr", 96, 128), [[0, 4], [1, 2], [0, 4]], 0, 0)
+    iota(v2("kr", 128, 160), [[16, 2], [0, 16]], 0, 1)
     iota(v2("vb1", 0, 128), [[32, 8], [1, 16]], -128, 0)
     iota(v2("ctb", 0, 32), [[1, 4], [64, 8]], 0, 0)
-    iota(v2("c8", 0, 32), [[0, 4], [1, 8]], 0, 0)
+    iota(v2("c8", 0, 32), [[0, 4], [16, 8]], 0, 0)
     iota(v2("q16", 0, 64), [[0, 4], [4, 16]], 0, 0)
     iota(v2("iof", 0, 128), [[up, 128]], START[rank], 0)
-    for h in range(2):
-        iota(half("plc", h), [[32, 8], [1, 16]], 256 * h - 256, 0)
 
-    def bits(n, sh, m, src="pc"):
-        ts(one(n), one(src), sh, A.arith_shift_right, m, A.bitwise_and)
-
+    fill(v2("wt", 0, 528), 0.0)
+    ts(one("m4"), one("p2"), 4, A.bitwise_and)
+    turn32(v2("kt", 0, 32), v2("kr", 0, 32))
+    cp(one("c0"), one("m4"))
     fill(v2("zt", 0, 512), 0.0)
-    bits("m4", 0, 3)
-    bits("pos", 3, 3)
-    fill(v2("w1t", 512, 1024), 0.0)
-    ts(one("c0"), one("m4"), 2.0, A.not_equal, 4.0, A.mult)
-    ts(one("c1"), one("m4"), 2.0, A.is_equal, 4.0, A.mult)
-    bits("b4", 4, 1)
-    fill(v2("sgn", 3, 16, 4), -1.0)
-    ts(v2("offg", 0, 8, 2), v2("io4", 0, 4), one("c0"), A.add)
-    ts(v2("offg", 1, 8, 2), v2("io4", 0, 4), one("c1"), A.add)
-    bits("r2", 2, 7, "p8")
-    ts(one("nz"), one("pos"), 0.5, A.is_lt, -1.0, A.add)
-    ts(one("k0"), one("pos"), 1.0, A.max, -256.0, A.mult)
-    ts(one("tp"), one("r2"), 2.5, A.is_lt, TINY, A.mult)
-    ts(one("h16"), one("b4"), 16.0, A.mult)
-    ts(one("kg"), one("nz"), 0.5, A.add, HIGH, A.mult)
-    ts(one("kk"), one("k0"), 1024.0, A.add)
+    ts(v2("offg", 0, 8), v2("io8", 0, 8), one("c0"), A.add)
     quant("xq", 256, 384, "zt", 0)
 
-    def planes(tile, src, t):
-        tt(v2(tile, 16 + t, 1024, 32), by(v2(src, 0, 8), v2("offg", 2 * t, 2 * t + 2)), v2("sgn", 0, 32), A.mult)
+    def planes(src, t):
+        tt(v2("wt", 16 + t, 528, 16), by(v2(src, 0, 8), v2("offg", 2 * t, 2 * t + 2)), v2("sgn", 0, 32), A.mult)
 
     def blank(win, c):
-        for a, b in ((896, 1153), (1281, 1409), (1537, 1665)):
+        for a, b in ((512, 769), (1025, 1153), (1409, 1537)):
             act(v2(win, a, b), v2("zt", 0, b - a), ACT.Identity, bias=c)
 
-    act(v2("w1t", 0, 512), v2("zt", 0, 512), ACT.Copy)
+    lin(one("nz"), one("pos"), -1.0, 0.0, ACT.Sign)
+    lin(one("tp"), one("pos"), TINY, -2 * TINY, ACT.Relu)
+    lin(one("kg"), one("nz"), HIGH, HIGH / 2)
+    lin(one("k0"), one("pos"), 1.0, -1.0, ACT.Relu)
     act(v2("n1", 256, 288), v2("zt", 0, 32), ACT.Copy)
+    lin(one("kk"), one("k0"), -384.0, float(START[0]))
     act(v2("d1", 256, 288), v2("zt", 0, 32), ACT.Copy)
     act(v2("d1", 0, 256), v2("zt", 0, 256), ACT.Identity, bias=one("nz"))
-    act(v2("val1", 0, 128), v2("vb1", 0, 128), ACT.Identity, bias=one("h16"))
+    lin(one("z1"), one("nz"), 1.0, 1.0)
     blank("win1", 128.0)
-    act(v2("f8", 0, 32), v2("c8", 0, 32), ACT.Sign)
-    for b in range(2):
-        act(v2("w2t", 512 * b, 512 * b + 512), v2("zt", 0, 512), ACT.Copy)
     for t in range(4):
-        planes("w1t", "plb", t)
+        planes("plb", t)
 
     quant("xq", 0, 128, "xb", 0)
-    quant("w1", 0, 128, "w1t", 0)
-    quant("w1", 128, 256, "w1t", 512)
+    quant("w1", 0, 132, "wt", 0)
     quant("xq", 128, 256, "xb", 512)
+    turn32(v2("kt", 32, 160), v2("kr", 32, 160))
     for h in range(2):
         for b in range(2):
-            mm(2 * h + b, 128, "w1", 128 * b, "xq", 128 * h)
+            mm(2 * h + b, 128, "w1", 4 * b, "xq", 128 * h)
+    act(v2("val1", 0, 128), v2("vb1", 0, 128), ACT.Identity, bias=one("h16"))
+    lin(one("mf"), one("bf"), one("z1"), 0.0)
+    act(v2("f8", 0, 32), v2("c8", 0, 32), ACT.Sign)
+    lin(one("nb"), one("bf"), -1.0, 1.0)
+    lin(one("k2"), one("kk"), one("bf"), 0.0)
+    for k in range(2):
+        lin(one("j%d" % k), one("mf"), JUMP[k], one("nz"))
+    lin(one("sc"), one("mf"), -1.0 * up, 0.0)
+    lin(one("cb"), one("mf"), 128.0 + up * START[rank], 0.0)
 
-    def gate(k, a, n, bank):
-        ts(v2("g%d" % k, a, a + n), v2("ps%d" % bank, 0, n), one("tp"), A.is_lt, one("kg"), A.mult)
+    def gate(k, a, n, bank, q="v"):
+        o, z = v2("g%d" % k, a, a + n), v2("ps%d" % bank, 0, n)
+        if q == "v":
+            ts(o, z, one("tp" if k == 1 else "t2"), A.is_lt, one("kg"), A.mult)
+        else:
+            lin(v2("sg", a, a + n), z, -1.0, one("bp"), ACT.Sign)
+            lin(o, v2("sg", a, a + n), one("kh"), one("kh"))
 
     def apart(k, a, n, bank):
         tt(v2("n%d" % k, a, a + n), v2("ps%d" % bank, 0, n), v2("g%d" % k, a, a + n), A.is_ge)
@@ -310,15 +322,19 @@ def rank_program(g, core, T, topo):
     scan(v2("v1", 0, 288), v2("n1", 0, 288), v2("d1", 0, 288), one("kk"), A.add, A.add)
     turn32(half("tn1", 1), half("n1", 1))
     turn32(v2("tv1", 0, 288), v2("v1", 0, 288))
+    planes("p2b", 0)
     scan(v2("r1", 0, 32), v2("tn1", 4, 256, 8), v2("tv1", 4, 256, 8), 0.0, A.mult, A.max)
-    bits("r8", 2, 7)
+    cp(v2("ends", 0, 4), v2("tv1", 260, 288, 8))
+    send("m0", [(r, v2("ends", r, r + 1), v2("nv", 4 * rank, 4 * rank + 1)) for r in off + near])
     ts(v2("do1", 0, 8), v2("r1", 3, 32, 4), -1.0, A.mult, float(TOP), A.add)
+    planes("p2b", 1)
     cp(by(v2("win1", 0, 1808), v2("do1", 0, 8)), v2("val1", 0, 128))
+    planes("p2b", 2)
 
     def listed(win, d):
         if d == 0:
-            return (T[win][:, 1023:895:-1], [(win, 896, 1024, 1, 1)], [])
-        return v2(win, 256 * d + 769, 256 * d + 897)
+            return (T[win][:, 639:511:-1], [(win, 512, 640, 1, 1)], [])
+        return v2(win, 384 * d + 257, 384 * d + 385)
 
     def spread(win, wd):
         for k in range(4):
@@ -333,81 +349,77 @@ def rank_program(g, core, T, topo):
         o = v2(offs, 8 * k, 8 * k + (b - a) // 16)
         if "c" in part:
             cp(codes(dst, a, b, dt.uint32), by(codes(src, 0, w, dt.uint32), o))
+        if "v" in part:
+            cp(plane(dst, a, b), by(plane(src, 0, w), o))
         if "s" in part:
             act(plane(dst, a, b), by(plane(src, 0, w), o), ACT.Copy)
 
-    spread("win1", "wd1")
-    for hf in range(2):
-        a, b = 16 * hf, 16 * hf + 16
-        turn32(v3("t21", a, b, 0, 32), v3("wd1", a, b, 0, 32))
-        if hf == 1:
-            bits("gi", 4, 7)
-        tt(v2("l1", a, b), v3i("t21", a, b, 0), v3i("t21", a, b, 16), A.add)
-        if hf == 1:
-            cp(one("gf"), one("gi"))
-        cp(v2("off1", a, b), v2("l1", a, b))
-        if hf == 0:
-            pick("slota", 0, 256, "xq", 384, "off1", 0)
-            send_cols(off, 0, "c1", "c1", "slota", "landa")
+    def wrap(k, a, step):
+        b = a + 16
+        if step == 0:
+            turn32(v3("t2%d" % k, a, b, 0, 32), v3("wd%d" % k, a, b, 0, 32))
+        elif step == 1:
+            tt(v2("l%d" % k, a, b), v3i("t2%d" % k, a, b, 0), v3i("t2%d" % k, a, b, 16), A.add)
         else:
-            ts(v2("dm1", 0, 32), v2("c8", 0, 32), one("gf"), A.is_equal)
-            pick("slota", 256, 384, "xq", 384, "off1", kn)
-            send_cols(near, 256, "c1", "c1", "slota", "landa")
+            cp(v2("off%d" % k, a, b), v2("l%d" % k, a, b))
 
-    def ends(a, b):
-        return v2("tv1", 260 + 8 * a, 253 + 8 * b, 8)
-
+    spread("win1", "wd1")
+    planes("p2b", 3)
+    wrap(1, 0, 0)
+    ts(v2("dm1", 0, 32), v2("c8", 0, 32), one("g16"), A.is_equal)
+    wrap(1, 0, 1)
+    ts(v2("offct", 0, 32), v2("ctb", 0, 32), one("q4"), A.add)
+    wrap(1, 0, 2)
+    ts(v2("dm2", 0, 64), v2("q16", 0, 64), one("q4"), A.is_equal)
+    pick("slota", 0, 256, "xq", 384, "off1", 0)
+    send_cols(off, 0, "c1", "s1", "slota", "landa")
+    wrap(1, 16, 0)
+    ts(v2("io2", 0, 128), v2("iof", 0, 128), one("mf"), A.mult)
+    wrap(1, 16, 1)
+    quant("w2", 0, 132, "wt", 0)
+    wrap(1, 16, 2)
+    lin(one("t2"), one("nb"), HIGH, one("tp"))
+    lin(one("lo"), one("k2"), 1.0, -128.0)
+    lin(one("kh"), one("kg"), 0.5, 0.0)
     tt(v2("pd1", 0, 32), v2("l1", 0, 32), v2("dm1", 0, 32), A.mult)
-    ts(one("mf"), one("r8"), 1.0, A.is_equal)
-    ts(v2("ea", 0, 1), ends(0, 1), -1.0, A.mult, START[0] + 128.0, A.add)
+    pick("slota", 256, 384, "xq", 384, "off1", kn)
+    send_cols(near, 256, "c1", "s1", "slota", "landa")
     scan(v2("pe1", 0, 32), v2("f8", 0, 32), v2("pd1", 0, 32), 0.0, A.mult, A.add)
-    for d in range(1, 4):
-        ts(v2("ea", d, d + 1), ends(d, d + 1), 128.0 - START[d], A.add)
-    for k in (0, 2):
-        ts(v2("msg", 4 * perm[k], 4 * perm[k + 1] + 1, 4 * (perm[k + 1] - perm[k])), v2("pe1", 8 * k + 7, 8 * k + 16, 8),
-           256.0 * rank, A.add)
-    ts(v2("eb", 0, 4), v2("ea", 0, 4), 0.0, A.max, one("mf"), A.mult)
-    ts(v2("msg", 1, 16, 4), ends(0, 4), one("mf"), A.mult)
-    bits("qi", 0, 15)
-    ts(v2("ec", 0, 4), v2("eb", 0, 4), 1.0, A.min, JUMP[rank], A.mult)
-    bits("b2", 2, 1)
-    ts(one("q4"), one("qi"), 4.0, A.mult)
-    tt(v2("msg", 2, 16, 4), v2("eb", 0, 4), v2("ec", 0, 4), A.add)
-    send("m1", [(r, v2("msg", 4 * r, 4 * r + 3), v2("nl", 4 * rank, 4 * rank + 3)) for r in off + near])
     pick("landa", 128 * rank, 128 * rank + 128, "xq", 384, "off1", ko)
-    cp(v2("nl", 4 * rank, 4 * rank + 3), v2("msg", 4 * rank, 4 * rank + 3))
-
-    def filled(s):
-        ts(half("d2", s), v2("io2", 0, 128), v2("nl", 4 * s + 1, 4 * s + 2), A.is_equal, one("j%d" % (s == 1)), A.mult)
+    ts(v2("msg", 0, 4), v2("pe1", 7, 32, 8), 256.0 * rank, A.add)
+    send("m1", [(r, v2("msg", perm.index(r), perm.index(r) + 1), slot_of("ida", rank)) for r in off + near])
 
     def to_row(s):
-        dma("s", "tb%d" % s, (T.tabrow[0:1, 128 * s:128 * s + 128], half("tabrow", s)[1], []), v2("nl", 4 * s, 4 * s + 1))
+        src = v2("msg", ko, ko + 1) if s == rank else (T.ida[s, :, 0], slot_of("ida", s)[1], [])
+        dma("s", "tb%d" % s, (T.tabrow[0:1, 128 * s:128 * s + 128], half("tabrow", s)[1], []), src)
 
+    dma("s", "zc", codes("hq", 512, 516, dt.uint8), codes("xq", 256, 260, dt.uint8))
+    dma("s", "zs", plane("hq", 512, 516), plane("xq", 256, 260))
     to_row(rank)
-    cp(one("bf"), one("b2"))
-    for k in range(2):
-        ts(one("j%d" % k), one("mf"), JUMP[k], A.mult, one("nz"), A.add)
-    fill(v2("tabrow", 512, 520), -1.0)
-    ts(one("k2"), one("kk"), one("bf"), A.mult)
-    ts(v2("offct", 0, 32), v2("ctb", 0, 32), one("q4"), A.add)
-    ts(v2("io2", 0, 128), v2("iof", 0, 128), one("mf"), A.mult)
-    ts(one("lo"), one("k2"), -128.0, A.add)
-    for t in range(4):
-        planes("w2t", "p2b", t)
+    for h in range(2):
+        iota(half("plc", h), [[32, 8], [1, 16]], 256 * h - 256, 0)
     quant("wvq", 0, 512, "wvb", 0)
-    quant("w2", 0, 256, "w2t", 0)
-    quant("hq", 512, 640, "zt", 0)
-    quant("wq", 0, 128, "wb", 0)
-    filled(rank)
-    ts(v2("dm2", 0, 64), v2("q16", 0, 64), one("q4"), A.is_equal)
+    for s in off + near:
+        arrive("m0", every, v2("nv", 4 * s, 4 * s + 1))
+    act(v2("nv", 4 * rank, 4 * rank + 1), v2("ends", rank, rank + 1), ACT.Copy)
+    lin(v2("ee", 0, 4), v2("nv", 0, 16, 4), one("mf"), 0.0)
+    lin(v2("eb", 0, 4), v2("nv", 0, 16, 4), one("sc"), one("cb"), ACT.Relu)
+    lin(one("bp"), one("t2"), 2.0, -TINY)
+    act(v2("ec", 0, 4), v2("eb", 0, 4), ACT.Sign)
+    lin(v2("tabrow", 512, 520), v2("zt", 0, 8), 1.0, -1.0)
+    for s in (0, 2, 1):
+        lin(v2("ed", s, s + 1), v2("ec", s, s + 1), JUMP[min(s, 1)], v2("eb", s, s + 1))
+    for s in range(4):
+        ts(half("d2", s), v2("io2", 0, 128), v2("ee", s, s + 1), A.is_equal, one("j%d" % min(s, 1)), A.mult)
+    tt(v2("d2", 128, 512, 256), v2("d2", 128, 512, 256), v2("ed", 0, 4, 2), A.subtract)
     act(v2("f16", 0, 64), v2("q16", 0, 64), ACT.Sign)
     act(v2("val2", 0, 256), v2("plc", 0, 256), ACT.Identity, bias=one("h16"))
     blank("win2", 256.0)
 
-    for s in range(N):
-        if s != rank:
-            arrive("c1", 2 * every, codes("landa", 128 * s, 128 * s + 128), plane("landa", 128 * s, 128 * s + 128))
-            arrive("m1", every, v2("nl", 4 * s, 4 * s + 3))
+    for s in off + near:
+        arrive("c1", every, codes("landa", 128 * s, 128 * s + 128))
+        arrive("s1", every, plane("landa", 128 * s, 128 * s + 128))
+        arrive("m1", every, slot_of("ida", s))
 
     def empty(q, tile, lo, t, bank, n, f):
         o, z = v2(tile, lo + t, lo + 4 * n, 4), v2("ps%d" % bank, 0, n)
@@ -418,7 +430,7 @@ def rank_program(g, core, T, topo):
         else:
             act(o, z, ACT.Copy, scale=0.0625) if q == "a" else ts(o, z, 0.0625, A.mult)
 
-    runs = ((0, 256), (256, 128), (384, 128))
+    sets = ((0, 8), (8, 12), (12, 16))
     free, held = list(range(8)), {}
 
     def take(key):
@@ -431,55 +443,51 @@ def rank_program(g, core, T, topo):
 
     for w in PLAN:
         c, z = w[:2], w[2:]
+        j = 0 if w == "tab" else int(w[3] if c == "mR" else w[2])
+        lo = 128 * j
         if w[0] == "p":
-            pick("ct", 128 * int(z[0]), 128 * int(z[1]) + 128, "landa", 512, "offct", int(z[0]), w[1])
+            pick("ct", lo, lo + 128, "landa", 512, "offct", j, "c" if c == "pc" else "s" if w[-1] == "a" else "v")
         elif c == "mV":
-            mm(take(w[1:]), 512, "ct", 128 * int(z), "wvq", 0)
+            mm(take(w[1:]), 512, "ct", lo, "wvq", 0)
         elif c == "eV":
-            empty(w[-1], "vt", 0, int(z[0]), drop(w[1:3]), 512, "copy")
+            empty(w[-1], "vt", 0, j, drop(w[1:3]), 512, "copy")
         elif c == "mA":
-            mm(take(w[1:]), 256, "ct", 128 * int(z[1]), "landa", 256 * int(z[0]))
+            mm(take(w[1:]), 256, "ct", 128 * int(z[1]), "landa", 256 * j)
         elif c == "eA":
-            empty(w[-1], "at", 1024 * int(z[0]), int(z[1]), drop(w[1:-1]), 256, "relu")
+            empty(w[-1], "at", 1024 * j, int(z[1]), drop(w[1:-1]), 256, "relu")
         elif c == "mH":
-            mm(take(w[1:]), runs[int(z[0])][1], "vq", 128 * int(z[1]), "aq", runs[int(z[0])][0])
+            mm(take(w[1:]), 128, "vq", 128 * int(z[1]), "aq", lo)
         elif c == "eH":
-            empty(w[-1], "ht", 4 * runs[int(z[0])][0], int(z[1]), drop(w[1:-1]), runs[int(z[0])][1], "scale")
+            empty(w[-1], "ht", 4 * lo, int(z[1]), drop(w[1:-1]), 128, "scale")
         elif c == "qv":
-            quant("vq", 0, 512, "vt", 0)
+            quant("vq", 2 * lo, 2 * lo + 256, "vt", 8 * lo)
         elif c == "qa":
-            quant("aq", 256 * int(z), 256 * int(z) + 256, "at", 1024 * int(z))
-        elif c == "fa":
-            if int(z) != rank:
-                filled(int(z))
+            quant("aq", 2 * lo, 2 * lo + 256, "at", 8 * lo)
+        elif c == "qh":
+            quant("hq", lo, lo + 128, "ht", 4 * lo)
+        elif c == "mR":
+            mm(take(w[1:]), 128, "w2", 4 * "ab".index(z[0]), "hq", lo)
+        elif c == "gR":
+            gate(2, lo, 128, drop("Ra%d" % j), w[-1])
+        elif c == "nR":
+            apart(2, lo, 128, drop("Rb%d" % j))
         elif c == "cR":
-            s = int(z)
-            ts(one("in%d" % s), v2("v2", 128 * s - 1, 128 * s), v2("nl", 4 * s - 2, 4 * s - 1), A.subtract, one("lo"), A.max)
+            ts(one("in2"), v2("v2", lo - 1, lo), v2("ed", j - 1, j), A.subtract, one("lo"), A.max)
         elif c == "sR":
-            s = int(z)
-            scan(half("v2", s), half("n2", s), half("d2", s), one("in%d" % s if s else "k2"), A.add, A.add)
+            scan(half("v2", j), half("n2", j), half("d2", j), v2("v2", lo - 1, lo) if j % 2 else one("in2" if j else "k2"),
+                 A.add, A.add)
+        elif c == "tn":
+            turn32(half("tn2", j), half("n2", j))
+        elif c == "tv":
+            turn32(half("tv2", j), half("v2", j))
         elif w == "tab":
             for s in off + near:
                 to_row(s)
             do("g", "partition_broadcast", v2("tab", 0, 520), (T.tabrow[0:1, 0:520], v2("tabrow", 0, 520)[1], []), 128)
         else:
-            j = int(z[-1])
-            lo, n = runs[j]
-            a, b = lo // 32, (lo + n) // 32
-            if c == "qh":
-                quant("hq", lo, lo + n, "ht", 4 * lo)
-            elif c == "mR":
-                mm(take(w[1:]), n, "w2", 128 * "ab".index(z[0]), "hq", lo)
-            elif c == "gR":
-                gate(2, lo, n, drop("Ra%d" % j))
-            elif c == "nR":
-                apart(2, lo, n, drop("Rb%d" % j))
-            elif c == "tn":
-                turn32(v2("tn2", lo, lo + n), v2("n2", lo, lo + n))
-            elif c == "tv":
-                turn32(v2("tv2", lo, lo + n), v2("v2", lo, lo + n))
-            elif c == "uR":
-                scan(v2("r2", 8 * a, 8 * b), v2("tn2", lo, lo + n, 4), v2("tv2", lo, lo + n, 4), 0.0, A.mult, A.max)
+            a, b = sets[j]
+            if c == "uR":
+                scan(v2("r2", 8 * a, 8 * b), v2("tn2", 32 * a, 32 * b, 4), v2("tv2", 32 * a, 32 * b, 4), 0.0, A.mult, A.max)
             elif c == "dR":
                 ts(v2("do2", a, b), v2("r2", 8 * a + 7, 8 * b, 8), -1.0, A.mult, float(TOP), A.add)
             else:
@@ -497,41 +505,35 @@ def rank_program(g, core, T, topo):
         else:
             scan(v2("gms", 16 * a, 16 * b), v2("f16", 16 * a, 16 * b), v2("gm", 16 * a, 16 * b), 0.0, A.mult, A.add)
 
-    def slot_of(s):
-        return (T.idd[s], [("idd", s, s + 1, 1, 1)], [])
-
     def send_numbers(rs):
-        send("m2", [(r, v2("gms", 16 * perm.index(r) + 15, 16 * perm.index(r) + 16), slot_of(rank)) for r in rs])
+        send("m2", [(r, v2("gms", 16 * perm.index(r) + 15, 16 * perm.index(r) + 16), slot_of("idd", rank)) for r in rs])
 
     spread("win2", "wd2")
-    turn32(v3("t22", 0, 16, 0, 32), v3("wd2", 0, 16, 0, 32))
-    tt(v2("l2", 0, 16), v3i("t22", 0, 16, 0), v3i("t22", 0, 16, 16), A.add)
-    cp(v2("off2", 0, 16), v2("l2", 0, 16))
+    for step in range(3):
+        wrap(2, 0, step)
     numbers(0, 2, 0)
-    pick("slotb", 0, 256, "hq", 640, "off2", 0)
+    pick("slotb", 0, 256, "hq", 516, "off2", 0)
     send_cols(off, 0, "c2_%d" % rank, "s2_%d" % rank, "slotb", "landb")
     numbers(0, 2, 1)
-    turn32(v3("t22", 16, 32, 0, 32), v3("wd2", 16, 32, 0, 32))
-    numbers(0, 2, 2)
-    tt(v2("l2", 16, 32), v3i("t22", 16, 32, 0), v3i("t22", 16, 32, 16), A.add)
-    numbers(0, 2, 3)
-    cp(v2("off2", 16, 32), v2("l2", 16, 32))
-    numbers(0, 2, 4)
+    for step in range(3):
+        wrap(2, 16, step)
+        numbers(0, 2, step + 2)
     numbers(2, 4, 0)
     send_numbers(off)
-    pick("slotb", 256, 384, "hq", 640, "off2", kn)
+    pick("slotb", 256, 384, "hq", 516, "off2", kn)
     send_cols(near, 256, "c2_%d" % rank, "s2_%d" % rank, "slotb", "landb")
     numbers(2, 4, 1)
-    pick("landb", 128 * rank, 128 * rank + 128, "hq", 640, "off2", ko)
-    for step in range(2, 5):
+    pick("landb", 128 * rank, 128 * rank + 128, "hq", 516, "off2", ko)
+    numbers(2, 4, 2)
+    quant("wq", 0, 128, "wb", 0)
+    for step in range(3, 5):
         numbers(2, 4, step)
     send_numbers(near)
 
-    for s in range(N):
-        if s != rank:
-            arrive("c2_%d" % s, share[s], codes("landb", 128 * s, 128 * s + 128))
-            arrive("s2_%d" % s, share[s], plane("landb", 128 * s, 128 * s + 128))
-            arrive("m2", every, slot_of(s))
+    for s in off + near:
+        arrive("c2_%d" % s, share[s], codes("landb", 128 * s, 128 * s + 128))
+        arrive("s2_%d" % s, share[s], plane("landb", 128 * s, 128 * s + 128))
+        arrive("m2", every, slot_of("idd", s))
 
     def store_codes(q, s):
         dma(q, "oc%d" % s, ext(T.oc[:, 512 * s:512 * s + 512]), codes("landb", 128 * s, 128 * s + 128, dt.uint8))
@@ -545,7 +547,7 @@ def rank_program(g, core, T, topo):
         dma(q, "yy%d" % s, ext(T.y[:, 128 * s:128 * s + 128]), half("yb", s))
 
     def store_id(q, s):
-        src = v2("gms", 16 * ko + 15, 16 * ko + 16) if s == rank else (T.idd[s, :, 0], slot_of(s)[1], [])
+        src = v2("gms", 16 * ko + 15, 16 * ko + 16) if s == rank else (T.idd[s, :, 0], slot_of("idd", s)[1], [])
         dma(q, "ii%d" % s, ext(T["id"][0:1, 128 * s:128 * s + 128]), src)
 
     store_codes("s", rank)

from concourse.bass import DstId, RemoteDMATransfer
from concourse.mybir import dt, AluOpType, ActivationFunctionType

F, B, I, U, H = "float32", "bfloat16", "int32", "uint16", "float16"
Q, S8 = "float8_e4m3fn_x4", "uint8"
COL = {n: ("ki", k) for k, n in enumerate(("p2", "m4"))}
COL.update({n: ("kf", k) for k, n in enumerate(("c0", "tp", "nz", "kg", "k0", "kk", "z1", "mf", "nb", "t2", "k2", "lo", "kh",
                                                "bp", "j0", "j1", "sc", "cb", "in2"))})
COL.update({n: ("kt", 32 * k) for k, n in enumerate(("pos", "h16", "q4", "bf", "g16"))})
SCRATCH = {"ida": ("dram", [4, 128, 1], F), "idd": ("dram", [4, 128, 1], F)}
for _n, _w, _t in (
        ("plb", 8, B), ("p2b", 8, B), ("xb", 1024, B), ("wvb", 2048, B), ("wb", 512, B),
        ("wt", 528, B), ("zt", 512, B), ("at", 2048, B), ("vt", 2048, B), ("ht", 2048, B),
        ("sgn", 32, B), ("val1", 128, B), ("val2", 256, B), ("win1", 1808, B), ("win2", 1808, B), ("ki", 4, I),
        ("kf", 24, F), ("kr", 160, F), ("kt", 160, F), ("io8", 8, F), ("vb1", 128, F), ("ctb", 32, F), ("plc", 256, F),
        ("c8", 32, F), ("dm1", 32, F), ("f8", 32, F), ("q16", 64, F), ("dm2", 64, F), ("f16", 64, F), ("iof", 128, F),
        ("io2", 128, H), ("eb", 4, F), ("ec", 4, F), ("ed", 4, F), ("ee", 4, F), ("tabrow", 520, F), ("tab", 520, F),
        ("ends", 4, F), ("msg", 4, F), ("nv", 16, F), ("sg", 512, B),
        ("g1", 256, B), ("n1", 288, B), ("d1", 288, B), ("v1", 288, H), ("tn1", 256, B), ("tv1", 288, H), ("r1", 32, F),
        ("l1", 32, F), ("l2", 32, F), ("pd1", 32, F), ("pe1", 32, F),
        ("g2", 512, B), ("n2", 512, B), ("d2", 512, H), ("v2", 512, H), ("tn2", 512, B), ("tv2", 512, H), ("r2", 128, F),
        ("pd", 32, F), ("pds", 32, F), ("gm", 64, F), ("gms", 64, F), ("yb", 512, F),
        ("offg", 8, U), ("do1", 8, U), ("do2", 16, U), ("off1", 32, U), ("off2", 32, U), ("offct", 32, U), ("offD", 4, U)):
    SCRATCH[_n] = ("sbuf", [128, _w], _t)
for _n in ("wd1", "t21", "wd2", "t22"):
    SCRATCH[_n] = ("sbuf", [128, 32, 32], B)
for _n, _w in (("w1", 132), ("xq", 384), ("slota", 384), ("landa", 512), ("ct", 512), ("wvq", 512), ("aq", 512), ("vq", 512),
               ("w2", 132), ("hq", 528), ("slotb", 384), ("landb", 512), ("wq", 128)):
    SCRATCH[_n + "c"] = ("sbuf", [128, _w], Q)
    SCRATCH[_n + "s"] = ("sbuf", [128, _w], S8)
for _k in range(8):
    SCRATCH["ps%d" % _k] = ("psum", [128, 512], F)

SEMAPHORES = (["sv", "sa", "sp", "sg", "sent", "c1", "s1", "m0", "m1", "m2", "lpl", "lx0", "lx1", "lp2", "lwv", "lw", "zc", "zs"]
              + ["%s_%d" % (n, k) for n in ("c2", "s2") for k in range(4)]
              + ["%s%d" % (n, k) for n in ("oc", "os", "yy", "ii", "tb") for k in range(4)])

TINY = 2.0 ** -120
HIGH = 2.0 ** 99
TOP = 1792
START = (1152, 1152, 768, 384)
JUMP = (384.0, 128.0)

PLAN = ("pc00 pc11 pc33 ps33v pc22 mV3 ps22a ps00a mV2 mA02 ps11a eV20a eV30v mV1 mV0 mA03 mA00 eV00a mA01 eA02v eV10v tab "
        "eA03v mA10 eA00v eA01a mA11 mA12 mA13 qv1 eA10a qa0 mH03 qv0 mH02 eA12a eA11v mH12 mH00 eA13a mH01 eH12a eH03v "
        "qa1 eH02v eH00a mH10 mH11 eH01a mH13 eH11v eH10v mH21 qh0 mH23 mH22 mH20 eH21v eH23v eH13a qh1 mH32 eH22a mH30 "
        "eH32v eH20a mRa0 mH33 gR0v eH30a eH33a mH31 mRa1 mRb0 qh2 eH31a gR1v mRb1 nR0 qh3 sR0 nR1 mRa2 tv0 tn0 mRa3 gR2a "
        "sR1 tn1 gR3v cR2 mRb2 mRb3 nR2 tv1 nR3 sR2 uR0 tn2 tn3 sR3 tv2 dR0 tv3 uR1 xR0 dR1 uR2 xR1 dR2 xR2").split()


def rank_program(g, core, T, topo):
    rank = T.rank_of(core)
    if rank is None:
        return
    N = len(T.cores)
    A, ACT = AluOpType, ActivationFunctionType
    eng = {"v": g.vector, "a": g.scalar, "p": g.tensor, "g": g, "s": g.sync}
    csem = {"v": "sv", "a": "sa", "p": "sp", "g": "sg"}
    total, waited, know, acc = {}, {}, {q: {} for q in eng}, {}

    def clash(x, y):
        if x[1] >= y[2] or y[1] >= x[2]:
            return False
        if x[3] == y[3] and x[3] > 1:
            a, b = x[1] % x[3], y[1] % y[3]
            return a < b + y[4] and b < a + x[4]
        return True

    def order(q, tok):
        sem, n, clock = tok
        k = know[q]
        if k.get(sem, 0) < n:
            eng[q].wait_ge(T.sem[sem], n)
            waited[sem] = max(waited.get(sem, 0), n)
            k[sem] = n
        for s, m in clock.items():
            if k.get(s, 0) < m:
                k[s] = m

    def touch(q, reads, writes):
        todo = []
        for kind, specs in ((0, reads), (1, writes)):
            for sp in specs:
                for old, okind, tok, oq in acc.get(sp[0], ()):
                    if SCRATCH[sp[0]][0] == "psum":
                        if oq != q:
                            todo.append(tok)
                    elif (kind or okind) and clash(sp, old):
                        todo.append(tok)
        todo.sort(key=lambda t: (t[0], -t[1]))
        for t in todo:
            order(q, t)

    def note(q, tok, reads, writes):
        for kind, specs in ((0, reads), (1, writes)):
            for sp in specs:
                acc.setdefault(sp[0], []).append((sp, kind, tok, q))

    def v2(name, a, b, step=1):
        return (T[name][:, a:b:step] if step > 1 else T[name][:, a:b], [(name, a, b, step, 1)], [])

    def half(name, h):
        return v2(name, 128 * h, 128 * h + 128)

    def one(n):
        return v2(COL[n][0], COL[n][1], COL[n][1] + 1)

    def v3(name, a, b, c, d):
        w = SCRATCH[name][1][2]
        return (T[name][:, a:b, c:d], [(name, a * w + c, (b - 1) * w + d, w, d - c)], [])

    def v3i(name, a, b, c):
        w = SCRATCH[name][1][2]
        return (T[name][:, a:b, c], [(name, a * w + c, (b - 1) * w + c + 1, w, 1)], [])

    def codes(name, a, b, bits=None):
        ap = T[name + "c"][:, a:b]
        return (ap.bitcast(bits) if bits else ap, [(name + "c", a, b, 1, 1)], [])

    def plane(name, a, b):
        return v2(name + "s", a, b)

    def slot_of(name, s):
        return (T[name][s], [(name, s, s + 1, 1, 1)], [])

    def by(win, off):
        return (win[0].indirect(off[0]), win[1], off[1])

    calls = {"tensor_copy": g.vector.tensor_copy, "tensor_tensor": g.vector.tensor_tensor, "memset": g.vector.memset,
             "tensor_scalar": g.vector.tensor_scalar,
             "tensor_tensor_scan": g.vector.tensor_tensor_scan, "transpose": g.vector.transpose,
             "quantize_mx": g.vector.quantize_mx, "activation": g.scalar.activation, "matmul_mx": g.tensor.matmul_mx,
             "iota": g.iota, "partition_broadcast": g.partition_broadcast}

    def do(q, call, *args, outs=1, **kw):
        reads, writes, plain = [], [], []
        for i, x in enumerate(args):
            if isinstance(x, tuple):
                (writes if i < outs else reads).extend(x[1])
                reads.extend(x[2])
                plain.append(x[0])
            else:
                plain.append(x)
        for k in kw:
            if isinstance(kw[k], tuple):
                reads.extend(kw[k][1])
                kw[k] = kw[k][0]
        touch(q, reads, writes)
        s = csem[q]
        calls[call](*plain, **kw).then_inc(T.sem[s], 1)
        total[s] = total.get(s, 0) + 1
        note(q, (s, total[s], dict(know[q])), reads, writes)

    def dma(q, sem, out, in_):
        touch(q, in_[1], out[1])
        eng[q].dma_start(out[0], in_[0]).then_inc(T.sem[sem], 16)
        total[sem] = 16
        note(q, (sem, 16, dict(know[q])), in_[1], out[1])

    def ext(ap):
        return (ap, [], [])

    def arrive(sem, n, *specs):
        total[sem] = n
        for sp in specs:
            note("far", (sem, n, {}), [], sp[1])

    def tt(out, a, b, op):
        do("v", "tensor_tensor", out, a, b, op)

    def ts(out, a, s1, op0, s2=None, op1=None):
        if op1 is None:
            do("v", "tensor_scalar", out, a, s1, None, op0)
        else:
            do("v", "tensor_scalar", out, a, s1, s2, op0, op1)

    def cp(out, a):
        do("v", "tensor_copy", out, a)

    def act(out, a, f, **kw):
        do("a", "activation", out, a, f, **kw)

    def lin(out, a, scale, bias, f=ACT.Identity):
        act(out, a, f, scale=scale, bias=bias)

    def fill(out, c):
        do("v", "memset", out, c)

    def scan(out, a, b, init, op0, op1):
        do("v", "tensor_tensor_scan", out, a, b, init, op0, op1)

    def turn32(out, a):
        do("v", "transpose", out, a)

    def quant(name, a, b, tile, lo):
        do("v", "quantize_mx", codes(name, a, b), plane(name, a, b), v2(tile, lo, lo + 4 * (b - a)), outs=2)

    def mm(bank, n, l, la, r, ra):
        do("p", "matmul_mx", v2("ps%d" % bank, 0, n), codes(l, la, la + 128), plane(l, la, la + 128),
           codes(r, ra, ra + n), plane(r, ra, ra + n), True, True)

    def iota(out, pattern, base, cm, flag=True):
        if flag:
            do("g", "iota", out, pattern, base, cm, allow_small_or_imprecise_dtypes=True)
        else:
            do("g", "iota", out, pattern, base, cm)

    off = [r for r in range(N) if r != rank and topo.chip(T.cores[r]) != topo.chip(core)]
    near = [r for r in range(N) if r != rank and topo.chip(T.cores[r]) == topo.chip(core)]
    perm = off + sorted(near + [rank])
    kn, ko = perm.index(near[0]), perm.index(rank)
    share = {r: 8 if r in near else 4 for r in off + near}
    every = sum(share.values())
    used, mask = [], {}
    for r in off + near:
        es = [e for e in topo.engines(core, T.cores[r]) if e not in used][:share[r]]
        used += es
        mask[r] = sum(1 << e for e in es)
    sent = [0]

    def send(sem, trio):
        trs = []
        for r, src, dst in trio:
            touch("g", src[1], [])
            rid, pid = topo.addr(T.cores[r])[:2]
            trs.append(RemoteDMATransfer(dst_ids=[DstId(rid=rid, pnc=pid)], dma_engine_mask=mask[r],
                                         remote_sem=T.sem[sem], src=src[0], dst=dst[0]))
            sent[0] += share[r]
        g.remote_dma_fused(trs, local_sem=T.sem.sent)

    def send_cols(rs, lo, sem, sem2, slot, land):
        u8 = dt.uint8
        at = [(r, lo + 128 * k) for k, r in enumerate(rs)]
        send(sem, [(r, codes(slot, c, c + 128, u8), codes(land, 128 * rank, 128 * rank + 128, u8)) for r, c in at])
        send(sem2, [(r, plane(slot, c, c + 128), plane(land, 128 * rank, 128 * rank + 128)) for r, c in at])

    dma("s", "lpl", v2("plb", 0, 8), ext(T.pl[:, 0:8]))
    dma("a", "lx0", v2("xb", 0, 512), ext(T.x[:, 0:512]))
    dma("s", "lx1", v2("xb", 512, 1024), ext(T.x[:, 512:1024]))
    touch("s", v2("xb", 0, 1024)[1], [])
    dma("s", "lp2", v2("p2b", 0, 8), ext(T.p2[:, 0:8]))
    dma("s", "lwv", v2("wvb", 0, 2048), ext(T.wv[:]))
    dma("s", "lw", v2("wb", 0, 512), ext(T.w[:]))

    up = 1 if rank == 0 else -1
    iota(one("p2"), [[0, 1]], 2, 2, False)
    iota(v2("kr", 0, 32), [[1, 4], [0, 8]], 0, 0)
    iota(v2("io8", 0, 8), [[1, 4], [0, 2]], 0, 0)
    iota(v2("sgn", 0, 32), [[0, 32]], 1, 0)
    iota(v2("sgn", 6, 32, 8), [[0, 4]], -1, 0)
    iota(v2("kr", 32, 64), [[16, 2], [0, 16]], 0, 0)
    iota(v2("kr", 64, 96), [[0, 2], [4, 16]], 0, 0)
    iota(v2("kr", 96, 128), [[0, 4], [1, 2], [0, 4]], 0, 0)
    iota(v2("kr", 128, 160), [[16, 2], [0, 16]], 0, 1)
    iota(v2("vb1", 0, 128), [[32, 8], [1, 16]], -128, 0)
    iota(v2("ctb", 0, 32), [[1, 4], [64, 8]], 0, 0)
    iota(v2("c8", 0, 32), [[0, 4], [16, 8]], 0, 0)
    iota(v2("q16", 0, 64), [[0, 4], [4, 16]], 0, 0)
    iota(v2("iof", 0, 128), [[up, 128]], START[rank], 0)

    fill(v2("wt", 0, 528), 0.0)
    ts(one("m4"), one("p2"), 4, A.bitwise_and)
    turn32(v2("kt", 0, 32), v2("kr", 0, 32))
    cp(one("c0"), one("m4"))
    fill(v2("zt", 0, 512), 0.0)
    ts(v2("offg", 0, 8), v2("io8", 0, 8), one("c0"), A.add)
    quant("xq", 256, 384, "zt", 0)

    def planes(src, t):
        tt(v2("wt", 16 + t, 528, 16), by(v2(src, 0, 8), v2("offg", 2 * t, 2 * t + 2)), v2("sgn", 0, 32), A.mult)

    def blank(win, c):
        for a, b in ((512, 769), (1025, 1153), (1409, 1537)):
            act(v2(win, a, b), v2("zt", 0, b - a), ACT.Identity, bias=c)

    lin(one("nz"), one("pos"), -1.0, 0.0, ACT.Sign)
    lin(one("tp"), one("pos"), TINY, -2 * TINY, ACT.Relu)
    lin(one("kg"), one("nz"), HIGH, HIGH / 2)
    lin(one("k0"), one("pos"), 1.0, -1.0, ACT.Relu)
    act(v2("n1", 256, 288), v2("zt", 0, 32), ACT.Copy)
    lin(one("kk"), one("k0"), -384.0, float(START[0]))
    act(v2("d1", 256, 288), v2("zt", 0, 32), ACT.Copy)
    act(v2("d1", 0, 256), v2("zt", 0, 256), ACT.Identity, bias=one("nz"))
    lin(one("z1"), one("nz"), 1.0, 1.0)
    blank("win1", 128.0)
    for t in range(4):
        planes("plb", t)

    quant("xq", 0, 128, "xb", 0)
    quant("w1", 0, 132, "wt", 0)
    quant("xq", 128, 256, "xb", 512)
    turn32(v2("kt", 32, 160), v2("kr", 32, 160))
    for h in range(2):
        for b in range(2):
            mm(2 * h + b, 128, "w1", 4 * b, "xq", 128 * h)
    act(v2("val1", 0, 128), v2("vb1", 0, 128), ACT.Identity, bias=one("h16"))
    lin(one("mf"), one("bf"), one("z1"), 0.0)
    act(v2("f8", 0, 32), v2("c8", 0, 32), ACT.Sign)
    lin(one("nb"), one("bf"), -1.0, 1.0)
    lin(one("k2"), one("kk"), one("bf"), 0.0)
    for k in range(2):
        lin(one("j%d" % k), one("mf"), JUMP[k], one("nz"))
    lin(one("sc"), one("mf"), -1.0 * up, 0.0)
    lin(one("cb"), one("mf"), 128.0 + up * START[rank], 0.0)

    def gate(k, a, n, bank, q="v"):
        o, z = v2("g%d" % k, a, a + n), v2("ps%d" % bank, 0, n)
        if q == "v":
            ts(o, z, one("tp" if k == 1 else "t2"), A.is_lt, one("kg"), A.mult)
        else:
            lin(v2("sg", a, a + n), z, -1.0, one("bp"), ACT.Sign)
            lin(o, v2("sg", a, a + n), one("kh"), one("kh"))

    def apart(k, a, n, bank):
        tt(v2("n%d" % k, a, a + n), v2("ps%d" % bank, 0, n), v2("g%d" % k, a, a + n), A.is_ge)

    gate(1, 0, 128, 0)
    gate(1, 128, 128, 2)
    apart(1, 0, 128, 1)
    apart(1, 128, 128, 3)
    turn32(half("tn1", 0), half("n1", 0))
    scan(v2("v1", 0, 288), v2("n1", 0, 288), v2("d1", 0, 288), one("kk"), A.add, A.add)
    turn32(half("tn1", 1), half("n1", 1))
    turn32(v2("tv1", 0, 288), v2("v1", 0, 288))
    planes("p2b", 0)
    scan(v2("r1", 0, 32), v2("tn1", 4, 256, 8), v2("tv1", 4, 256, 8), 0.0, A.mult, A.max)
    cp(v2("ends", 0, 4), v2("tv1", 260, 288, 8))
    send("m0", [(r, v2("ends", r, r + 1), v2("nv", 4 * rank, 4 * rank + 1)) for r in off + near])
    ts(v2("do1", 0, 8), v2("r1", 3, 32, 4), -1.0, A.mult, float(TOP), A.add)
    planes("p2b", 1)
    cp(by(v2("win1", 0, 1808), v2("do1", 0, 8)), v2("val1", 0, 128))
    planes("p2b", 2)

    def listed(win, d):
        if d == 0:
            return (T[win][:, 639:511:-1], [(win, 512, 640, 1, 1)], [])
        return v2(win, 384 * d + 257, 384 * d + 385)

    def spread(win, wd):
        for k in range(4):
            for h in range(2):
                o, z = v3(wd, 8 * k, 8 * k + 8, 16 * h, 16 * h + 16), listed(win, perm[k])
                if k > 1 or k + h == 0:
                    act(o, z, ACT.Copy)
                else:
                    cp(o, z)

    def pick(dst, a, b, src, w, offs, k, part="cs"):
        o = v2(offs, 8 * k, 8 * k + (b - a) // 16)
        if "c" in part:
            cp(codes(dst, a, b, dt.uint32), by(codes(src, 0, w, dt.uint32), o))
        if "v" in part:
            cp(plane(dst, a, b), by(plane(src, 0, w), o))
        if "s" in part:
            act(plane(dst, a, b), by(plane(src, 0, w), o), ACT.Copy)

    def wrap(k, a, step):
        b = a + 16
        if step == 0:
            turn32(v3("t2%d" % k, a, b, 0, 32), v3("wd%d" % k, a, b, 0, 32))
        elif step == 1:
            tt(v2("l%d" % k, a, b), v3i("t2%d" % k, a, b, 0), v3i("t2%d" % k, a, b, 16), A.add)
        else:
            cp(v2("off%d" % k, a, b), v2("l%d" % k, a, b))

    spread("win1", "wd1")
    planes("p2b", 3)
    wrap(1, 0, 0)
    ts(v2("dm1", 0, 32), v2("c8", 0, 32), one("g16"), A.is_equal)
    wrap(1, 0, 1)
    ts(v2("offct", 0, 32), v2("ctb", 0, 32), one("q4"), A.add)
    wrap(1, 0, 2)
    ts(v2("dm2", 0, 64), v2("q16", 0, 64), one("q4"), A.is_equal)
    pick("slota", 0, 256, "xq", 384, "off1", 0)
    send_cols(off, 0, "c1", "s1", "slota", "landa")
    wrap(1, 16, 0)
    ts(v2("io2", 0, 128), v2("iof", 0, 128), one("mf"), A.mult)
    wrap(1, 16, 1)
    quant("w2", 0, 132, "wt", 0)
    wrap(1, 16, 2)
    lin(one("t2"), one("nb"), HIGH, one("tp"))
    lin(one("lo"), one("k2"), 1.0, -128.0)
    lin(one("kh"), one("kg"), 0.5, 0.0)
    tt(v2("pd1", 0, 32), v2("l1", 0, 32), v2("dm1", 0, 32), A.mult)
    pick("slota", 256, 384, "xq", 384, "off1", kn)
    send_cols(near, 256, "c1", "s1", "slota", "landa")
    scan(v2("pe1", 0, 32), v2("f8", 0, 32), v2("pd1", 0, 32), 0.0, A.mult, A.add)
    pick("landa", 128 * rank, 128 * rank + 128, "xq", 384, "off1", ko)
    ts(v2("msg", 0, 4), v2("pe1", 7, 32, 8), 256.0 * rank, A.add)
    send("m1", [(r, v2("msg", perm.index(r), perm.index(r) + 1), slot_of("ida", rank)) for r in off + near])

    def to_row(s):
        src = v2("msg", ko, ko + 1) if s == rank else (T.ida[s, :, 0], slot_of("ida", s)[1], [])
        dma("s", "tb%d" % s, (T.tabrow[0:1, 128 * s:128 * s + 128], half("tabrow", s)[1], []), src)

    dma("s", "zc", codes("hq", 512, 516, dt.uint8), codes("xq", 256, 260, dt.uint8))
    dma("s", "zs", plane("hq", 512, 516), plane("xq", 256, 260))
    to_row(rank)
    for h in range(2):
        iota(half("plc", h), [[32, 8], [1, 16]], 256 * h - 256, 0)
    quant("wvq", 0, 512, "wvb", 0)
    for s in off + near:
        arrive("m0", every, v2("nv", 4 * s, 4 * s + 1))
    act(v2("nv", 4 * rank, 4 * rank + 1), v2("ends", rank, rank + 1), ACT.Copy)
    lin(v2("ee", 0, 4), v2("nv", 0, 16, 4), one("mf"), 0.0)
    lin(v2("eb", 0, 4), v2("nv", 0, 16, 4), one("sc"), one("cb"), ACT.Relu)
    lin(one("bp"), one("t2"), 2.0, -TINY)
    act(v2("ec", 0, 4), v2("eb", 0, 4), ACT.Sign)
    lin(v2("tabrow", 512, 520), v2("zt", 0, 8), 1.0, -1.0)
    for s in (0, 2, 1):
        lin(v2("ed", s, s + 1), v2("ec", s, s + 1), JUMP[min(s, 1)], v2("eb", s, s + 1))
    for s in range(4):
        ts(half("d2", s), v2("io2", 0, 128), v2("ee", s, s + 1), A.is_equal, one("j%d" % min(s, 1)), A.mult)
    tt(v2("d2", 128, 512, 256), v2("d2", 128, 512, 256), v2("ed", 0, 4, 2), A.subtract)
    act(v2("f16", 0, 64), v2("q16", 0, 64), ACT.Sign)
    act(v2("val2", 0, 256), v2("plc", 0, 256), ACT.Identity, bias=one("h16"))
    blank("win2", 256.0)

    for s in off + near:
        arrive("c1", every, codes("landa", 128 * s, 128 * s + 128))
        arrive("s1", every, plane("landa", 128 * s, 128 * s + 128))
        arrive("m1", every, slot_of("ida", s))

    def empty(q, tile, lo, t, bank, n, f):
        o, z = v2(tile, lo + t, lo + 4 * n, 4), v2("ps%d" % bank, 0, n)
        if f == "copy":
            act(o, z, ACT.Copy) if q == "a" else cp(o, z)
        elif f == "relu":
            act(o, z, ACT.Relu, scale=0.0625) if q == "a" else ts(o, z, 0.0, A.max, 0.0625, A.mult)
        else:
            act(o, z, ACT.Copy, scale=0.0625) if q == "a" else ts(o, z, 0.0625, A.mult)

    sets = ((0, 8), (8, 12), (12, 16))
    free, held = list(range(8)), {}

    def take(key):
        held[key] = free.pop(0)
        return held[key]

    def drop(key):
        free.append(held[key])
        return held[key]

    for w in PLAN:
        c, z = w[:2], w[2:]
        j = 0 if w == "tab" else int(w[3] if c == "mR" else w[2])
        lo = 128 * j
        if w[0] == "p":
            pick("ct", lo, lo + 128, "landa", 512, "offct", j, "c" if c == "pc" else "s" if w[-1] == "a" else "v")
        elif c == "mV":
            mm(take(w[1:]), 512, "ct", lo, "wvq", 0)
        elif c == "eV":
            empty(w[-1], "vt", 0, j, drop(w[1:3]), 512, "copy")
        elif c == "mA":
            mm(take(w[1:]), 256, "ct", 128 * int(z[1]), "landa", 256 * j)
        elif c == "eA":
            empty(w[-1], "at", 1024 * j, int(z[1]), drop(w[1:-1]), 256, "relu")
        elif c == "mH":
            mm(take(w[1:]), 128, "vq", 128 * int(z[1]), "aq", lo)
        elif c == "eH":
            empty(w[-1], "ht", 4 * lo, int(z[1]), drop(w[1:-1]), 128, "scale")
        elif c == "qv":
            quant("vq", 2 * lo, 2 * lo + 256, "vt", 8 * lo)
        elif c == "qa":
            quant("aq", 2 * lo, 2 * lo + 256, "at", 8 * lo)
        elif c == "qh":
            quant("hq", lo, lo + 128, "ht", 4 * lo)
        elif c == "mR":
            mm(take(w[1:]), 128, "w2", 4 * "ab".index(z[0]), "hq", lo)
        elif c == "gR":
            gate(2, lo, 128, drop("Ra%d" % j), w[-1])
        elif c == "nR":
            apart(2, lo, 128, drop("Rb%d" % j))
        elif c == "cR":
            ts(one("in2"), v2("v2", lo - 1, lo), v2("ed", j - 1, j), A.subtract, one("lo"), A.max)
        elif c == "sR":
            scan(half("v2", j), half("n2", j), half("d2", j), v2("v2", lo - 1, lo) if j % 2 else one("in2" if j else "k2"),
                 A.add, A.add)
        elif c == "tn":
            turn32(half("tn2", j), half("n2", j))
        elif c == "tv":
            turn32(half("tv2", j), half("v2", j))
        elif w == "tab":
            for s in off + near:
                to_row(s)
            do("g", "partition_broadcast", v2("tab", 0, 520), (T.tabrow[0:1, 0:520], v2("tabrow", 0, 520)[1], []), 128)
        else:
            a, b = sets[j]
            if c == "uR":
                scan(v2("r2", 8 * a, 8 * b), v2("tn2", 32 * a, 32 * b, 4), v2("tv2", 32 * a, 32 * b, 4), 0.0, A.mult, A.max)
            elif c == "dR":
                ts(v2("do2", a, b), v2("r2", 8 * a + 7, 8 * b, 8), -1.0, A.mult, float(TOP), A.add)
            else:
                cp(by(v2("win2", 0, 1808), v2("do2", a, b)), v2("val2", 16 * a, 16 * b))

    def numbers(a, b, step):
        if step == 0:
            tt(v2("pd", 8 * a, 8 * b), v2("l2", 8 * a, 8 * b), v2("dm1", 8 * a, 8 * b), A.mult)
        elif step == 1:
            scan(v2("pds", 8 * a, 8 * b), v2("f8", 8 * a, 8 * b), v2("pd", 8 * a, 8 * b), 0.0, A.mult, A.add)
        elif step == 2:
            cp(v2("offD", a, b), v2("pds", 8 * a + 7, 8 * b, 8))
        elif step == 3:
            tt(v2("gm", 16 * a, 16 * b), by(v2("tab", 0, 520), v2("offD", a, b)), v2("dm2", 16 * a, 16 * b), A.mult)
        else:
            scan(v2("gms", 16 * a, 16 * b), v2("f16", 16 * a, 16 * b), v2("gm", 16 * a, 16 * b), 0.0, A.mult, A.add)

    def send_numbers(rs):
        send("m2", [(r, v2("gms", 16 * perm.index(r) + 15, 16 * perm.index(r) + 16), slot_of("idd", rank)) for r in rs])

    spread("win2", "wd2")
    for step in range(3):
        wrap(2, 0, step)
    numbers(0, 2, 0)
    pick("slotb", 0, 256, "hq", 516, "off2", 0)
    send_cols(off, 0, "c2_%d" % rank, "s2_%d" % rank, "slotb", "landb")
    numbers(0, 2, 1)
    for step in range(3):
        wrap(2, 16, step)
        numbers(0, 2, step + 2)
    numbers(2, 4, 0)
    send_numbers(off)
    pick("slotb", 256, 384, "hq", 516, "off2", kn)
    send_cols(near, 256, "c2_%d" % rank, "s2_%d" % rank, "slotb", "landb")
    numbers(2, 4, 1)
    pick("landb", 128 * rank, 128 * rank + 128, "hq", 516, "off2", ko)
    numbers(2, 4, 2)
    quant("wq", 0, 128, "wb", 0)
    for step in range(3, 5):
        numbers(2, 4, step)
    send_numbers(near)

    for s in off + near:
        arrive("c2_%d" % s, share[s], codes("landb", 128 * s, 128 * s + 128))
        arrive("s2_%d" % s, share[s], plane("landb", 128 * s, 128 * s + 128))
        arrive("m2", every, slot_of("idd", s))

    def store_codes(q, s):
        dma(q, "oc%d" % s, ext(T.oc[:, 512 * s:512 * s + 512]), codes("landb", 128 * s, 128 * s + 128, dt.uint8))

    def product(q, s, bank):
        mm(bank, 128, "wq", 0, "landb", 128 * s)
        o, z = v2("yb", 128 * s, 128 * s + 128), v2("ps%d" % bank, 0, 128)
        act(o, z, ACT.Copy) if q == "a" else cp(o, z)

    def store_y(q, s):
        dma(q, "yy%d" % s, ext(T.y[:, 128 * s:128 * s + 128]), half("yb", s))

    def store_id(q, s):
        src = v2("gms", 16 * ko + 15, 16 * ko + 16) if s == rank else (T.idd[s, :, 0], slot_of("idd", s)[1], [])
        dma(q, "ii%d" % s, ext(T["id"][0:1, 128 * s:128 * s + 128]), src)

    store_codes("s", rank)
    product("a", rank, free[0])
    store_y("a", rank)
    store_id("s", rank)
    for s in off:
        store_codes("s", s)
    store_codes("a", near[0])
    product("a", near[0], free[1])
    store_y("a", near[0])
    product("a", off[0], free[2])
    product("v", off[1], free[3])
    for k in range(4):
        dma("s", "os%d" % k, ext(T.osc[4 * k:4 * k + 4, :]),
            (T.landbs[32 * k:32 * k + 4, 0:512], plane("landb", 0, 512)[1], []))
    store_y("a", off[0])
    store_y("s", off[1])
    for i, s in enumerate(off + near):
        store_id("as"[i % 2], s)
    total["sent"] = sent[0]
    for sem in SEMAPHORES:
        if total.get(sem, 0) > waited.get(sem, 0):
            g.wait_ge(T.sem[sem], total[sem])
